import numpy as np
import ml_dtypes


def mxq(x, axis, fmt="e4m3"):
    dtype, down = {"e4m3": (ml_dtypes.float8_e4m3fn, 7), "e5m2": (ml_dtypes.float8_e5m2, 14)}[fmt]
    v = np.moveaxis(np.asarray(x, np.float32).astype(ml_dtypes.bfloat16).astype(np.float64), axis, -1)
    blocks = v.reshape(v.shape[:-1] + (-1, 32))
    amax = np.abs(blocks).max(-1, keepdims=True)
    byte = np.maximum(np.where(amax > 0, np.frexp(amax)[1] - 1 + 127, 0) - down, 1)
    scale = np.exp2(byte - 127.0)
    codes = (blocks / scale).astype(np.float32).astype(dtype).astype(np.float64)
    return np.moveaxis((codes * scale).reshape(v.shape), -1, axis)


WIDE = False


def mx_kscale(k):
    if not WIDE:
        return np.ones(k)
    levels = np.array([10, -10, 5, -5, 0])
    if k % 512:
        return np.exp2(np.random.permutation(np.resize(levels, k // 32))).repeat(32)
    a = np.empty((k // 512, 16))
    for p in range(k // 512):
        a[p, :8] = np.random.permutation(np.resize(levels, 8))
        for g in range(8):
            far = levels[np.abs(levels - a[p, g]) >= 10]
            a[p, g + 8] = far[np.random.randint(len(far))]
    return np.exp2(a.ravel()).repeat(32)


def f64(x):
    return np.asarray(x).astype(np.float64)


def striped(idx):
    return np.tile(idx.reshape(-1, 16).T, (8, 1)).astype(np.uint16)


def unstriped(offs):
    return offs[:16].T.reshape(-1).astype(np.int64)


def gelu(v):
    return 0.5 * v * (1.0 + np.tanh(np.sqrt(2.0 / np.pi) * (v + 0.044715 * v**3)))


K, T, D, S, V, H, N = 1024, 2048, 3, 768, 384, 512, 128


def setup_inputs():
    n = np.random.standard_normal
    s = mx_kscale(K)[:, None]
    u = mx_kscale(H)
    return {
        "xT": (n((K, T)) * s).astype(np.float32),
        "w1": (n((K, H)) / np.sqrt(K) / s * u).astype(np.float32),
        "w2": (n((H, N)) / np.sqrt(H) / u[:, None]).astype(np.float32),
        "gate": np.tile(np.random.uniform(0.2, 1.0, (D, 1, V)) / np.sqrt(D), (1, N, 1)).astype(np.float32),
        "offs": striped(np.random.permutation(T)[:S]),
        "pos1": striped(np.random.permutation(S)[:V]),
        "pos2": striped(np.random.permutation(S)[:V]),
        "pos3": striped(np.random.permutation(S)[:V]),
    }


def reference(xT, w1, w2, gate, offs, pos1, pos2, pos3):
    idx = unstriped(offs)
    xq = mxq(f64(xT)[:, idx], 0, "e4m3")
    h = gelu(mxq(f64(w1), 0, "e4m3").T @ xq)
    y = mxq(f64(w2), 0, "e4m3").T @ mxq(h, 0, "e4m3")
    return sum(f64(gate[d]) * y[:, unstriped(p)] for d, p in enumerate((pos1, pos2, pos3)))

@@ -1,0 +1,235 @@
+from contextlib import ExitStack
+
+import concourse.mybir as mybir
+
+K, T, D, S, V, H, N = 1024, 2048, 3, 768, 384, 512, 128
+FLOPS = 2 * K * H * S + 2 * H * N * S
+
+F32 = mybir.dt.float32
+BF16 = mybir.dt.bfloat16
+U32 = mybir.dt.uint32
+U16 = mybir.dt.uint16
+U8 = mybir.dt.uint8
+FP8X4 = mybir.dt.float8_e4m3fn_x4
+MULT = mybir.AluOpType.mult
+GELU = mybir.ActivationFunctionType.Gelu_apprx_tanh
+
+P = 128
+PACK = 4
+K_PASS = P * PACK
+PASSES = K // K_PASS
+SLICE = 128
+SLICES = S // SLICE
+
+
+def tile_picked_sub_mlp_gelu_sub_e_kernel(
+    tc, xT, w1, w2, gate, offs, pos1, pos2, pos3, out
+):
+    nc = tc.nc
+    with ExitStack() as ctx:
+        keep = ctx.enter_context(tc.tile_pool(name="keep", bufs=1))
+        banks = ctx.enter_context(tc.psum_pool(name="banks", bufs=1))
+
+        dummy = keep.tile([P, 1], F32, name="dummy")
+        nc.vector.memset(dummy[:], 0.0)
+        dummy_out = keep.tile([P, 1], F32, name="dummy_out")
+        nc.scalar.activation(dummy_out[:], dummy[:], GELU)
+
+        planes = []
+        offsets = keep.tile([P, S // 16], U16, name="offsets")
+        for s in range(PASSES):
+            rows = xT[s * K_PASS : (s + 1) * K_PASS, :].rearrange("(p t) c -> p t c", t=PACK)
+            for t in range(PACK):
+                plane = keep.tile([P, T], F32, name=f"plane{s}{t}")
+                nc.sync.dma_start(plane[:], rows[:, t, :])
+                planes.append(plane)
+                if s == 0 and t == 0:
+                    nc.sync.dma_start(offsets[:], offs)
+        w1_raw = []
+        for s in range(PASSES):
+            rows = w1[s * K_PASS : (s + 1) * K_PASS, :].rearrange("(p j) c -> p j c", j=PACK)
+            for u in range(2):
+                raw = keep.tile([P, 2, H], F32, name=f"w1raw{s}{u}")
+                nc.sync.dma_start(raw[:], rows[:, 2 * u : 2 * u + 2, :])
+                w1_raw.append(raw)
+        w2_raw = keep.tile([P, PACK, N], F32, name="w2_raw")
+        nc.sync.dma_start(w2_raw[:], w2.rearrange("(p j) n -> p j n", j=PACK))
+        places = []
+        for d, pos in enumerate((pos1, pos2, pos3)):
+            place = keep.tile([P, V // 16], U16, name=f"place{d}")
+            nc.sync.dma_start(place[:], pos)
+            places.append(place)
+        gates = keep.tile([P, D, V], F32, name="gates")
+        nc.sync.dma_start(gates[:], gate.rearrange("d m v -> m d v"))
+
+        x_codes = []
+        x_scales = []
+        for s in range(PASSES):
+            x_codes.append(keep.tile([P, S], U32, align_bytes=64, name=f"x_codes{s}"))
+            x_scales.append(keep.tile([P, S], U8, align_bytes=64, name=f"x_scales{s}"))
+
+        def quantise_x(s, grouped, a, b):
+            nc.vector.quantize_mx(
+                out=x_codes[s][:, a:b].bitcast(FP8X4),
+                scales=x_scales[s][:, a:b],
+                in_=grouped[:, a:b, :].rearrange("p n t -> p (n t)"),
+            )
+
+        xg0 = keep.tile([P, S, PACK], BF16, align_bytes=64, name="xg0")
+        xg1 = keep.tile([P, S, PACK], BF16, align_bytes=64, name="xg1")
+        picked0 = keep.tile([P, PACK, S], F32, name="picked0")
+        picked1 = keep.tile([P, 2, S], F32, name="picked1")
+        for t in range(PACK):
+            nc.vector.tensor_copy(picked0[:, t, :], planes[t][:].indirect(offsets[:]))
+        nc.scalar.copy(
+            xg0[:].rearrange("p (c i) t -> p c t i", i=4),
+            picked0[:].rearrange("p t (c i) -> p c t i", i=4),
+        )
+        for t in range(2):
+            nc.vector.tensor_copy(picked1[:, t, :], planes[4 + t][:].indirect(offsets[:]))
+        nc.scalar.copy(xg1[:, :, 0:2], picked1[:].rearrange("p t n -> p n t"))
+        quantise_x(0, xg0, 0, 512)
+        quantise_x(0, xg0, 512, 768)
+        nc.vector.tensor_copy(xg1[:, :, 2], planes[6][:].indirect(offsets[:]))
+        nc.vector.tensor_copy(xg1[:, 0:512, 3], planes[7][:].indirect(offsets[:, 0:32]))
+
+        w1_codes = []
+        w1_scales = []
+        w1_grouped = []
+        for s in range(PASSES):
+            w1_codes.append(keep.tile([P, H], U32, align_bytes=64, name=f"w1_codes{s}"))
+            w1_scales.append(keep.tile([P, H], U8, align_bytes=64, name=f"w1_scales{s}"))
+            w1_grouped.append(keep.tile([P, PACK, P, PACK], BF16, align_bytes=64, name=f"w1_grouped{s}"))
+
+        def group_w1(copy, s, u, a, b):
+            raw = w1_raw[2 * s + u][:].rearrange("p j (m t) -> p m t j", t=PACK)
+            copy(
+                w1_grouped[s][:, a:b, :, 2 * u : 2 * u + 2].rearrange("p t m j -> p m t j"),
+                raw[:, :, a:b, :],
+            )
+
+        def quantise_w1(s):
+            for a, b in ((0, 2), (2, 4)):
+                nc.vector.quantize_mx(
+                    out=w1_codes[s][:, P * a : P * b].bitcast(FP8X4),
+                    scales=w1_scales[s][:, P * a : P * b],
+                    in_=w1_grouped[s][:, a:b].rearrange("p t m j -> p (t m j)"),
+                )
+
+        def gpsimd_copy(dst, src):
+            nc.gpsimd.tensor_scalar(dst, src, 1.0, 0.0, MULT, mybir.AluOpType.add)
+
+        group_w1(gpsimd_copy, 0, 0, 0, 4)
+        group_w1(nc.scalar.copy, 0, 1, 0, 4)
+        quantise_x(1, xg1, 0, 512)
+        quantise_w1(0)
+        group_w1(nc.vector.tensor_copy, 1, 0, 0, 2)
+        group_w1(nc.scalar.copy, 1, 0, 2, 4)
+        group_w1(nc.scalar.copy, 1, 1, 2, 4)
+        group_w1(nc.vector.tensor_copy, 1, 1, 0, 2)
+        quantise_w1(1)
+        nc.vector.tensor_copy(xg1[:, 512:768, 3], planes[7][:].indirect(offsets[:, 32:48]))
+
+        quantise_x(1, xg1, 512, 768)
+
+        acc = []
+        for i in range(SLICES):
+            acc.append(banks.tile([P, PACK, SLICE], F32, name=f"acc{i}", tag=f"acc{i}"))
+
+        def layer1(i, t, s):
+            cols = slice(i * SLICE, (i + 1) * SLICE)
+            nc.tensor.matmul_mx(
+                out=acc[i][:, t, :],
+                lhsT=w1_codes[s][:, t * P : (t + 1) * P].bitcast(FP8X4),
+                lhsT_scale=w1_scales[s][:, t * P : (t + 1) * P],
+                rhs=x_codes[s][:, cols].bitcast(FP8X4),
+                rhs_scale=x_scales[s][:, cols],
+                start=(s == 0),
+                stop=(s == PASSES - 1),
+            )
+
+        for r in range(3):
+            warm = banks.tile([P, 512], F32, name="warm", tag="y1")
+            nc.tensor.matmul_mx(
+                out=warm[:],
+                lhsT=x_codes[0][:, 0:P].bitcast(FP8X4),
+                lhsT_scale=x_scales[0][:, 0:P],
+                rhs=x_codes[1][:, 0:512].bitcast(FP8X4),
+                rhs_scale=x_scales[1][:, 0:512],
+                start=True,
+                stop=True,
+            )
+        w2_grouped = keep.tile([P, N, PACK], BF16, align_bytes=64, name="w2_grouped")
+        w2_codes = keep.tile([P, N], U32, align_bytes=64, name="w2_codes")
+        w2_scales = keep.tile([P, N], U8, align_bytes=64, name="w2_scales")
+        for i in range(SLICES):
+            layer1(i, 0, 0)
+        hidden = []
+        for i in range(SLICES):
+            layer1(i, 0, 1)
+            for t in range(1, PACK):
+                for s in range(PASSES):
+                    layer1(i, t, s)
+            h = keep.tile([P, SLICE, PACK], BF16, align_bytes=64, name=f"h{i}")
+            nc.scalar.activation(h[:], acc[i][:].rearrange("p t n -> p n t"), GELU)
+            h_codes = keep.tile([P, SLICE], U32, align_bytes=64, name=f"h_codes{i}")
+            h_scales = keep.tile([P, SLICE], U8, align_bytes=64, name=f"h_scales{i}")
+            nc.vector.quantize_mx(
+                out=h_codes[:].bitcast(FP8X4),
+                scales=h_scales[:],
+                in_=h[:].rearrange("p n t -> p (n t)"),
+            )
+            hidden.append((h_codes, h_scales))
+            if i == 1:
+                nc.vector.tensor_copy(w2_grouped[:], w2_raw[:].rearrange("p j n -> p n j"))
+            if i == 2:
+                nc.vector.quantize_mx(
+                    out=w2_codes[:].bitcast(FP8X4),
+                    scales=w2_scales[:],
+                    in_=w2_grouped[:].rearrange("p n j -> p (n j)"),
+                )
+
+        y = keep.tile([P, S], F32, name="y")
+        y_main = banks.tile([P, 4, SLICE], F32, name="y_main", tag="y0")
+        y_fifth = banks.tile([P, SLICE], F32, name="y_fifth", tag="y1")
+        y_last = banks.tile([P, SLICE], F32, name="y_last", tag="acc0")
+        y_parts = [y_main[:, i, :] for i in range(4)] + [y_fifth[:], y_last[:]]
+        for i in range(SLICES):
+            h_codes, h_scales = hidden[i]
+            nc.tensor.matmul_mx(
+                out=y_parts[i],
+                lhsT=w2_codes[:].bitcast(FP8X4),
+                lhsT_scale=w2_scales[:],
+                rhs=h_codes[:].bitcast(FP8X4),
+                rhs_scale=h_scales[:],
+                start=True,
+                stop=True,
+            )
+        nc.scalar.copy(y[:, 0 : 4 * SLICE], y_main[:].rearrange("p i n -> p (i n)"))
+        nc.vector.tensor_copy(y[:, 4 * SLICE : 5 * SLICE], y_fifth[:])
+        nc.scalar.copy(y[:, 5 * SLICE : 6 * SLICE], y_last[:])
+
+        terms = []
+        for d in range(D):
+            term = keep.tile([P, V], F32, name=f"term{d}")
+            terms.append(term)
+        part = keep.tile([P, V], F32, name="part")
+        total = keep.tile([P, V], F32, name="total")
+        halves = (slice(0, V // 2), slice(V // 2, V))
+
+        def fetch(d, cols):
+            nc.vector.tensor_tensor(
+                terms[d][:, cols],
+                y[:].indirect(places[d][:, cols.start // 16 : cols.stop // 16]),
+                gates[:, d, cols],
+                MULT,
+            )
+
+        fetch(0, slice(0, V))
+        fetch(1, slice(0, V))
+        fetch(2, halves[0])
+        nc.vector.tensor_add(part[:], terms[0][:], terms[1][:])
+        fetch(2, halves[1])
+        for cols in halves:
+            nc.vector.tensor_add(total[:, cols], part[:, cols], terms[2][:, cols])
+            nc.sync.dma_start(out[:, cols], total[:, cols])

@@ -12,6 +12,7 @@ U16 = mybir.dt.uint16
 U8 = mybir.dt.uint8
 FP8X4 = mybir.dt.float8_e4m3fn_x4
 MULT = mybir.AluOpType.mult
+ADD = mybir.AluOpType.add
 GELU = mybir.ActivationFunctionType.Gelu_apprx_tanh
 
 P = 128
@@ -20,6 +21,8 @@ K_PASS = P * PACK
 PASSES = K // K_PASS
 SLICE = 128
 SLICES = S // SLICE
+THIRD = S // 3
+M_SPLIT = 84
 
 
 def tile_picked_sub_mlp_gelu_sub_e_kernel(
@@ -35,23 +38,28 @@ def tile_picked_sub_mlp_gelu_sub_e_kernel(
         dummy_out = keep.tile([P, 1], F32, name="dummy_out")
         nc.scalar.activation(dummy_out[:], dummy[:], GELU)
 
-        planes = []
-        offsets = keep.tile([P, S // 16], U16, name="offsets")
-        for s in range(PASSES):
+        def load_plane(s, t):
             rows = xT[s * K_PASS : (s + 1) * K_PASS, :].rearrange("(p t) c -> p t c", t=PACK)
-            for t in range(PACK):
-                plane = keep.tile([P, T], F32, name=f"plane{s}{t}")
-                nc.sync.dma_start(plane[:], rows[:, t, :])
-                planes.append(plane)
-                if s == 0 and t == 0:
-                    nc.sync.dma_start(offsets[:], offs)
-        w1_raw = []
-        for s in range(PASSES):
-            rows = w1[s * K_PASS : (s + 1) * K_PASS, :].rearrange("(p j) c -> p j c", j=PACK)
-            for u in range(2):
-                raw = keep.tile([P, 2, H], F32, name=f"w1raw{s}{u}")
-                nc.sync.dma_start(raw[:], rows[:, 2 * u : 2 * u + 2, :])
-                w1_raw.append(raw)
+            plane = keep.tile([P, T], F32, align_bytes=64, name=f"plane{s}{t}", tag=f"plane{s}{t}")
+            nc.sync.dma_start(plane[:], rows[:, t, :])
+            return plane
+
+        def w1_rows(s):
+            return w1[s * K_PASS : (s + 1) * K_PASS, :].rearrange("(p j) c -> p j c", j=PACK)
+
+        planes = [load_plane(0, 0)]
+        offsets = keep.tile([P, S // 16], U16, name="offsets")
+        nc.sync.dma_start(offsets[:], offs)
+        for t in range(1, PACK):
+            planes.append(load_plane(0, t))
+        w1_raw0 = keep.tile([P, PACK, H], F32, name="w1_raw0")
+        nc.sync.dma_start(w1_raw0[:], w1_rows(0))
+        for t in range(PACK):
+            planes.append(load_plane(1, t))
+        w1_raw1a = keep.tile([P, 2, H], F32, name="w1_raw1a")
+        nc.sync.dma_start(w1_raw1a[:], w1_rows(1)[:, 0:2, :])
+        w1_raw1b = keep.tile([P, 2, H], F32, align_bytes=64, name="w1_raw1b", tag="late")
+        nc.sync.dma_start(w1_raw1b[:], w1_rows(1)[:, 2:4, :])
         w2_raw = keep.tile([P, PACK, N], F32, name="w2_raw")
         nc.sync.dma_start(w2_raw[:], w2.rearrange("(p j) n -> p j n", j=PACK))
         places = []
@@ -62,152 +70,136 @@ def tile_picked_sub_mlp_gelu_sub_e_kernel(
         gates = keep.tile([P, D, V], F32, name="gates")
         nc.sync.dma_start(gates[:], gate.rearrange("d m v -> m d v"))
 
+        def quantise(codes, scales, grouped):
+            nc.vector.quantize_mx(out=codes.bitcast(FP8X4), scales=scales, in_=grouped)
+
+        def entries(a, b):
+            return offsets[:, a // 16 : b // 16]
+
+        def weave_all(copy, dst, src):
+            copy(
+                dst.rearrange("p (c i) t -> p c t i", i=4),
+                src.rearrange("p t (c i) -> p c t i", i=4),
+            )
+
+        def gpsimd_copy(dst, src):
+            nc.gpsimd.tensor_scalar(dst, src, 1.0, 0.0, MULT, ADD)
+
         x_codes = []
         x_scales = []
         for s in range(PASSES):
             x_codes.append(keep.tile([P, S], U32, align_bytes=64, name=f"x_codes{s}"))
             x_scales.append(keep.tile([P, S], U8, align_bytes=64, name=f"x_scales{s}"))
 
-        def quantise_x(s, grouped, a, b):
-            nc.vector.quantize_mx(
-                out=x_codes[s][:, a:b].bitcast(FP8X4),
-                scales=x_scales[s][:, a:b],
-                in_=grouped[:, a:b, :].rearrange("p n t -> p (n t)"),
-            )
-
         xg0 = keep.tile([P, S, PACK], BF16, align_bytes=64, name="xg0")
-        xg1 = keep.tile([P, S, PACK], BF16, align_bytes=64, name="xg1")
-        picked0 = keep.tile([P, PACK, S], F32, name="picked0")
-        picked1 = keep.tile([P, 2, S], F32, name="picked1")
-        for t in range(PACK):
-            nc.vector.tensor_copy(picked0[:, t, :], planes[t][:].indirect(offsets[:]))
-        nc.scalar.copy(
-            xg0[:].rearrange("p (c i) t -> p c t i", i=4),
-            picked0[:].rearrange("p t (c i) -> p c t i", i=4),
-        )
+        picked01 = keep.tile([P, 2, S], F32, name="picked01")
+        picked23 = keep.tile([P, 2, S], F32, name="picked23")
         for t in range(2):
-            nc.vector.tensor_copy(picked1[:, t, :], planes[4 + t][:].indirect(offsets[:]))
-        nc.scalar.copy(xg1[:, :, 0:2], picked1[:].rearrange("p t n -> p n t"))
-        quantise_x(0, xg0, 0, 512)
-        quantise_x(0, xg0, 512, 768)
-        nc.vector.tensor_copy(xg1[:, :, 2], planes[6][:].indirect(offsets[:]))
-        nc.vector.tensor_copy(xg1[:, 0:512, 3], planes[7][:].indirect(offsets[:, 0:32]))
+            nc.vector.tensor_copy(picked01[:, t, :], planes[t][:].indirect(offsets[:]))
+        nc.scalar.copy(xg0[:, :, 0:2], picked01[:].rearrange("p t n -> p n t"))
+        for t in range(2):
+            nc.vector.tensor_copy(picked23[:, t, :], planes[2 + t][:].indirect(offsets[:]))
+        for c in range(3):
+            cols = slice(c * THIRD, (c + 1) * THIRD)
+            copy = nc.vector.tensor_copy if c == 0 else nc.scalar.copy
+            copy(xg0[:, cols, 2:4], picked23[:, :, cols].rearrange("p t n -> p n t"))
+        w1_grouped0 = keep.tile([P, PACK, P, PACK], BF16, align_bytes=64, name="w1_grouped0")
+        raw0 = w1_raw0[:].rearrange("p j (m t) -> p m j t", t=PACK)
+        grouped0 = w1_grouped0[:].rearrange("p t m j -> p m j t")
+        nc.scalar.copy(grouped0, raw0)
+        for c in range(3):
+            cols = slice(c * THIRD, (c + 1) * THIRD)
+            quantise(x_codes[0][:, cols], x_scales[0][:, cols], xg0[:, cols, :].rearrange("p n t -> p (n t)"))
 
-        w1_codes = []
-        w1_scales = []
-        w1_grouped = []
-        for s in range(PASSES):
-            w1_codes.append(keep.tile([P, H], U32, align_bytes=64, name=f"w1_codes{s}"))
-            w1_scales.append(keep.tile([P, H], U8, align_bytes=64, name=f"w1_scales{s}"))
-            w1_grouped.append(keep.tile([P, PACK, P, PACK], BF16, align_bytes=64, name=f"w1_grouped{s}"))
+        picked1 = keep.tile([P, PACK, S], F32, name="picked1")
+        xg1a = keep.tile([P, THIRD, PACK], BF16, align_bytes=64, name="xg1a")
+        nc.vector.tensor_copy(picked1[:, 0, :], planes[4][:].indirect(offsets[:]))
+        w1_codes0 = keep.tile([P, H], U32, align_bytes=64, name="w1_codes0", tag="plane10")
+        w1_scales0 = keep.tile([P, H], U8, align_bytes=64, name="w1_scales0")
+        quantise(w1_codes0[:], w1_scales0[:], w1_grouped0[:].rearrange("p t m j -> p (t m j)"))
+        nc.vector.tensor_copy(picked1[:, 1, :], planes[5][:].indirect(offsets[:]))
+        nc.scalar.copy(xg1a[:, :, 0:2], picked1[:, 0:2, 0:THIRD].rearrange("p t n -> p n t"))
+        for t in (2, 3):
+            nc.vector.tensor_copy(xg1a[:, :, t], planes[4 + t][:].indirect(entries(0, THIRD)))
+            nc.vector.tensor_copy(picked1[:, t, THIRD:S], planes[4 + t][:].indirect(entries(THIRD, S)))
+        quantise(x_codes[1][:, 0:THIRD], x_scales[1][:, 0:THIRD], xg1a[:].rearrange("p n t -> p (n t)"))
 
-        def group_w1(copy, s, u, a, b):
-            raw = w1_raw[2 * s + u][:].rearrange("p j (m t) -> p m t j", t=PACK)
-            copy(
-                w1_grouped[s][:, a:b, :, 2 * u : 2 * u + 2].rearrange("p t m j -> p m t j"),
-                raw[:, :, a:b, :],
+        w1_codes1 = keep.tile([P, H], U32, align_bytes=64, name="w1_codes1")
+        w1_scales1 = keep.tile([P, H], U8, align_bytes=64, name="w1_scales1")
+        w1_grouped1 = keep.tile([P, PACK, P, PACK], BF16, align_bytes=64, name="w1_grouped1")
+        grouped1 = w1_grouped1[:].rearrange("p t m j -> p m j t")
+        raw1a = w1_raw1a[:].rearrange("p j (m t) -> p m j t", t=PACK)
+        raw1b = w1_raw1b[:].rearrange("p j (m t) -> p m j t", t=PACK)
+        gpsimd_copy(
+            grouped1[:, M_SPLIT:P, 0:2, :].rearrange("p m j t -> p m t j"),
+            raw1a[:, M_SPLIT:P].rearrange("p m j t -> p m t j"),
+        )
+        nc.scalar.copy(grouped1[:, 0:M_SPLIT, 0:2, :], raw1a[:, 0:M_SPLIT])
+        nc.vector.tensor_copy(grouped1[:, 0:M_SPLIT, 2:4, :], raw1b[:, 0:M_SPLIT])
+        nc.scalar.copy(grouped1[:, M_SPLIT:P, 2:4, :], raw1b[:, M_SPLIT:P])
+        for a, b in ((0, 2), (2, 4)):
+            quantise(
+                w1_codes1[:, P * a : P * b],
+                w1_scales1[:, P * a : P * b],
+                w1_grouped1[:, a:b].rearrange("p t m j -> p (t m j)"),
             )
+        xg1bc = keep.tile([P, 2 * THIRD, PACK], BF16, align_bytes=64, name="xg1bc", tag="late")
+        weave_all(nc.scalar.copy, xg1bc[:, 0:THIRD, :], picked1[:, :, THIRD : 2 * THIRD])
+        weave_all(nc.vector.tensor_copy, xg1bc[:, THIRD : 2 * THIRD, :], picked1[:, :, 2 * THIRD : S])
+        for c in (1, 2):
+            cols = slice(c * THIRD, (c + 1) * THIRD)
+            src = xg1bc[:, (c - 1) * THIRD : c * THIRD, :]
+            quantise(x_codes[1][:, cols], x_scales[1][:, cols], src.rearrange("p n t -> p (n t)"))
+        w2_grouped = keep.tile([P, N, PACK], BF16, align_bytes=64, name="w2_grouped")
+        w2_codes = keep.tile([P, N], U32, align_bytes=64, name="w2_codes")
+        w2_scales = keep.tile([P, N], U8, align_bytes=64, name="w2_scales")
+        weave_all(nc.vector.tensor_copy, w2_grouped[:], w2_raw[:])
+        quantise(w2_codes[:], w2_scales[:], w2_grouped[:].rearrange("p n j -> p (n j)"))
 
-        def quantise_w1(s):
-            for a, b in ((0, 2), (2, 4)):
-                nc.vector.quantize_mx(
-                    out=w1_codes[s][:, P * a : P * b].bitcast(FP8X4),
-                    scales=w1_scales[s][:, P * a : P * b],
-                    in_=w1_grouped[s][:, a:b].rearrange("p t m j -> p (t m j)"),
-                )
-
-        def gpsimd_copy(dst, src):
-            nc.gpsimd.tensor_scalar(dst, src, 1.0, 0.0, MULT, mybir.AluOpType.add)
-
-        group_w1(gpsimd_copy, 0, 0, 0, 4)
-        group_w1(nc.scalar.copy, 0, 1, 0, 4)
-        quantise_x(1, xg1, 0, 512)
-        quantise_w1(0)
-        group_w1(nc.vector.tensor_copy, 1, 0, 0, 2)
-        group_w1(nc.scalar.copy, 1, 0, 2, 4)
-        group_w1(nc.scalar.copy, 1, 1, 2, 4)
-        group_w1(nc.vector.tensor_copy, 1, 1, 0, 2)
-        quantise_w1(1)
-        nc.vector.tensor_copy(xg1[:, 512:768, 3], planes[7][:].indirect(offsets[:, 32:48]))
-
-        quantise_x(1, xg1, 512, 768)
-
+        w1_codes = (w1_codes0, w1_codes1)
+        w1_scales = (w1_scales0, w1_scales1)
         acc = []
         for i in range(SLICES):
             acc.append(banks.tile([P, PACK, SLICE], F32, name=f"acc{i}", tag=f"acc{i}"))
 
-        def layer1(i, t, s):
+        def layer1(i, s):
             cols = slice(i * SLICE, (i + 1) * SLICE)
-            nc.tensor.matmul_mx(
-                out=acc[i][:, t, :],
-                lhsT=w1_codes[s][:, t * P : (t + 1) * P].bitcast(FP8X4),
-                lhsT_scale=w1_scales[s][:, t * P : (t + 1) * P],
-                rhs=x_codes[s][:, cols].bitcast(FP8X4),
-                rhs_scale=x_scales[s][:, cols],
-                start=(s == 0),
-                stop=(s == PASSES - 1),
-            )
-
-        for r in range(3):
-            warm = banks.tile([P, 512], F32, name="warm", tag="y1")
-            nc.tensor.matmul_mx(
-                out=warm[:],
-                lhsT=x_codes[0][:, 0:P].bitcast(FP8X4),
-                lhsT_scale=x_scales[0][:, 0:P],
-                rhs=x_codes[1][:, 0:512].bitcast(FP8X4),
-                rhs_scale=x_scales[1][:, 0:512],
-                start=True,
-                stop=True,
-            )
-        w2_grouped = keep.tile([P, N, PACK], BF16, align_bytes=64, name="w2_grouped")
-        w2_codes = keep.tile([P, N], U32, align_bytes=64, name="w2_codes")
-        w2_scales = keep.tile([P, N], U8, align_bytes=64, name="w2_scales")
-        for i in range(SLICES):
-            layer1(i, 0, 0)
-        hidden = []
-        for i in range(SLICES):
-            layer1(i, 0, 1)
-            for t in range(1, PACK):
-                for s in range(PASSES):
-                    layer1(i, t, s)
-            h = keep.tile([P, SLICE, PACK], BF16, align_bytes=64, name=f"h{i}")
-            nc.scalar.activation(h[:], acc[i][:].rearrange("p t n -> p n t"), GELU)
-            h_codes = keep.tile([P, SLICE], U32, align_bytes=64, name=f"h_codes{i}")
-            h_scales = keep.tile([P, SLICE], U8, align_bytes=64, name=f"h_scales{i}")
-            nc.vector.quantize_mx(
-                out=h_codes[:].bitcast(FP8X4),
-                scales=h_scales[:],
-                in_=h[:].rearrange("p n t -> p (n t)"),
-            )
-            hidden.append((h_codes, h_scales))
-            if i == 1:
-                nc.vector.tensor_copy(w2_grouped[:], w2_raw[:].rearrange("p j n -> p n j"))
-            if i == 2:
-                nc.vector.quantize_mx(
-                    out=w2_codes[:].bitcast(FP8X4),
-                    scales=w2_scales[:],
-                    in_=w2_grouped[:].rearrange("p n j -> p (n j)"),
+            for t in range(PACK):
+                nc.tensor.matmul_mx(
+                    out=acc[i][:, t, :],
+                    lhsT=w1_codes[s][:, t * P : (t + 1) * P].bitcast(FP8X4),
+                    lhsT_scale=w1_scales[s][:, t * P : (t + 1) * P],
+                    rhs=x_codes[s][:, cols].bitcast(FP8X4),
+                    rhs_scale=x_scales[s][:, cols],
+                    start=(s == 0 and t == 0),
+                    stop=(s == PASSES - 1 and t == PACK - 1),
                 )
 
-        y = keep.tile([P, S], F32, name="y")
-        y_main = banks.tile([P, 4, SLICE], F32, name="y_main", tag="y0")
-        y_fifth = banks.tile([P, SLICE], F32, name="y_fifth", tag="y1")
-        y_last = banks.tile([P, SLICE], F32, name="y_last", tag="acc0")
-        y_parts = [y_main[:, i, :] for i in range(4)] + [y_fifth[:], y_last[:]]
         for i in range(SLICES):
-            h_codes, h_scales = hidden[i]
+            layer1(i, 0)
+        h = keep.tile([P, S, PACK], BF16, align_bytes=64, name="h")
+        for i in range(SLICES):
+            layer1(i, 1)
+            nc.scalar.activation(h[:, i * SLICE : (i + 1) * SLICE, :], acc[i][:].rearrange("p t n -> p n t"), GELU)
+
+        h_codes = keep.tile([P, S], U32, align_bytes=64, name="h_codes")
+        h_scales = keep.tile([P, S], U8, align_bytes=64, name="h_scales")
+        y = keep.tile([P, S], F32, name="y")
+        batches = ((0, 256, "y0"), (256, 512, "y1"), (512, 640, "acc0"), (640, 768, "acc1"))
+        for a, b, tag in batches:
+            quantise(h_codes[:, a:b], h_scales[:, a:b], h[:, a:b, :].rearrange("p n t -> p (n t)"))
+            y_part = banks.tile([P, b - a], F32, name=f"y_part{a}", tag=tag)
             nc.tensor.matmul_mx(
-                out=y_parts[i],
+                out=y_part[:],
                 lhsT=w2_codes[:].bitcast(FP8X4),
                 lhsT_scale=w2_scales[:],
-                rhs=h_codes[:].bitcast(FP8X4),
-                rhs_scale=h_scales[:],
+                rhs=h_codes[:, a:b].bitcast(FP8X4),
+                rhs_scale=h_scales[:, a:b],
                 start=True,
                 stop=True,
             )
-        nc.scalar.copy(y[:, 0 : 4 * SLICE], y_main[:].rearrange("p i n -> p (i n)"))
-        nc.vector.tensor_copy(y[:, 4 * SLICE : 5 * SLICE], y_fifth[:])
-        nc.scalar.copy(y[:, 5 * SLICE : 6 * SLICE], y_last[:])
+            copy = nc.scalar.copy if b == S else nc.vector.tensor_copy
+            copy(y[:, a:b], y_part[:])
 
         terms = []
         for d in range(D):

@@ -23,6 +23,8 @@ SLICE = 128
 SLICES = S // SLICE
 THIRD = S // 3
 M_SPLIT = 84
+M_SPLIT0 = 40
+WARM = 4
 
 
 def tile_picked_sub_mlp_gelu_sub_e_kernel(
@@ -101,22 +103,23 @@ def tile_picked_sub_mlp_gelu_sub_e_kernel(
             nc.vector.tensor_copy(picked23[:, t, :], planes[2 + t][:].indirect(offsets[:]))
         for c in range(3):
             cols = slice(c * THIRD, (c + 1) * THIRD)
-            copy = nc.vector.tensor_copy if c == 0 else nc.scalar.copy
+            copy = nc.vector.tensor_copy if c < 2 else nc.scalar.copy
             copy(xg0[:, cols, 2:4], picked23[:, :, cols].rearrange("p t n -> p n t"))
         w1_grouped0 = keep.tile([P, PACK, P, PACK], BF16, align_bytes=64, name="w1_grouped0")
         raw0 = w1_raw0[:].rearrange("p j (m t) -> p m j t", t=PACK)
         grouped0 = w1_grouped0[:].rearrange("p t m j -> p m j t")
-        nc.scalar.copy(grouped0, raw0)
+        nc.scalar.copy(grouped0[:, M_SPLIT0:P], raw0[:, M_SPLIT0:P])
         for c in range(3):
             cols = slice(c * THIRD, (c + 1) * THIRD)
             quantise(x_codes[0][:, cols], x_scales[0][:, cols], xg0[:, cols, :].rearrange("p n t -> p (n t)"))
+        nc.vector.tensor_copy(grouped0[:, 0:M_SPLIT0], raw0[:, 0:M_SPLIT0])
+        w1_codes0 = keep.tile([P, H], U32, align_bytes=64, name="w1_codes0")
+        w1_scales0 = keep.tile([P, H], U8, align_bytes=64, name="w1_scales0")
+        quantise(w1_codes0[:], w1_scales0[:], w1_grouped0[:].rearrange("p t m j -> p (t m j)"))
 
         picked1 = keep.tile([P, PACK, S], F32, name="picked1")
         xg1a = keep.tile([P, THIRD, PACK], BF16, align_bytes=64, name="xg1a")
         nc.vector.tensor_copy(picked1[:, 0, :], planes[4][:].indirect(offsets[:]))
-        w1_codes0 = keep.tile([P, H], U32, align_bytes=64, name="w1_codes0", tag="plane10")
-        w1_scales0 = keep.tile([P, H], U8, align_bytes=64, name="w1_scales0")
-        quantise(w1_codes0[:], w1_scales0[:], w1_grouped0[:].rearrange("p t m j -> p (t m j)"))
         nc.vector.tensor_copy(picked1[:, 1, :], planes[5][:].indirect(offsets[:]))
         nc.scalar.copy(xg1a[:, :, 0:2], picked1[:, 0:2, 0:THIRD].rearrange("p t n -> p n t"))
         for t in (2, 3):
@@ -177,6 +180,17 @@ def tile_picked_sub_mlp_gelu_sub_e_kernel(
 
         for i in range(SLICES):
             layer1(i, 0)
+        warm = banks.tile([P, THIRD], F32, name="warm", tag="y1")
+        for r in range(WARM):
+            nc.tensor.matmul_mx(
+                out=warm[:],
+                lhsT=w1_codes0[:, 0:P].bitcast(FP8X4),
+                lhsT_scale=w1_scales0[:, 0:P],
+                rhs=x_codes[1][:, 0:THIRD].bitcast(FP8X4),
+                rhs_scale=x_scales[1][:, 0:THIRD],
+                start=True,
+                stop=True,
+            )
         h = keep.tile([P, S, PACK], BF16, align_bytes=64, name="h")
         for i in range(SLICES):
             layer1(i, 1)

@@ -138,8 +138,9 @@ def tile_picked_sub_mlp_gelu_sub_e_kernel(
             raw1a[:, M_SPLIT:P].rearrange("p m j t -> p m t j"),
         )
         nc.scalar.copy(grouped1[:, 0:M_SPLIT, 0:2, :], raw1a[:, 0:M_SPLIT])
-        nc.vector.tensor_copy(grouped1[:, 0:M_SPLIT, 2:4, :], raw1b[:, 0:M_SPLIT])
-        nc.scalar.copy(grouped1[:, M_SPLIT:P, 2:4, :], raw1b[:, M_SPLIT:P])
+        for a, b in ((0, 2), (2, 4)):
+            nc.vector.tensor_copy(grouped1[:, 0:M_SPLIT, 2:4, a:b], raw1b[:, 0:M_SPLIT, :, a:b])
+            nc.scalar.copy(grouped1[:, M_SPLIT:P, 2:4, a:b], raw1b[:, M_SPLIT:P, :, a:b])
         for a, b in ((0, 2), (2, 4)):
             quantise(
                 w1_codes1[:, P * a : P * b],
@@ -212,7 +213,7 @@ def tile_picked_sub_mlp_gelu_sub_e_kernel(
                 start=True,
                 stop=True,
             )
-            copy = nc.scalar.copy if b == S else nc.vector.tensor_copy
+            copy = nc.scalar.copy if b - a == SLICE else nc.vector.tensor_copy
             copy(y[:, a:b], y_part[:])
 
         terms = []

@@ -141,7 +141,7 @@ def tile_picked_sub_mlp_gelu_sub_e_kernel(
         for a, b in ((0, 2), (2, 4)):
             nc.vector.tensor_copy(grouped1[:, 0:M_SPLIT, 2:4, a:b], raw1b[:, 0:M_SPLIT, :, a:b])
             nc.scalar.copy(grouped1[:, M_SPLIT:P, 2:4, a:b], raw1b[:, M_SPLIT:P, :, a:b])
-        for a, b in ((0, 2), (2, 4)):
+        for a, b in ((0, 2), (2, 3), (3, 4)):
             quantise(
                 w1_codes1[:, P * a : P * b],
                 w1_scales1[:, P * a : P * b],
@@ -195,12 +195,16 @@ def tile_picked_sub_mlp_gelu_sub_e_kernel(
         h = keep.tile([P, S, PACK], BF16, align_bytes=64, name="h")
         for i in range(SLICES):
             layer1(i, 1)
-            nc.scalar.activation(h[:, i * SLICE : (i + 1) * SLICE, :], acc[i][:].rearrange("p t n -> p n t"), GELU)
+            pieces = ((0, SLICE),) if i < SLICES - 1 else ((0, SLICE // 2), (SLICE // 2, SLICE))
+            for a, b in pieces:
+                nc.scalar.activation(
+                    h[:, i * SLICE + a : i * SLICE + b, :], acc[i][:, :, a:b].rearrange("p t n -> p n t"), GELU, bias=dummy_out[:]
+                )
 
         h_codes = keep.tile([P, S], U32, align_bytes=64, name="h_codes")
         h_scales = keep.tile([P, S], U8, align_bytes=64, name="h_scales")
         y = keep.tile([P, S], F32, name="y")
-        batches = ((0, 256, "y0"), (256, 512, "y1"), (512, 640, "acc0"), (640, 768, "acc1"))
+        batches = ((0, 256, "y0"), (256, 512, "y1"), (512, 640, "acc0"), (640, 704, "acc1"), (704, 768, "acc2"))
         for a, b, tag in batches:
             quantise(h_codes[:, a:b], h_scales[:, a:b], h[:, a:b, :].rearrange("p n t -> p (n t)"))
             y_part = banks.tile([P, b - a], F32, name=f"y_part{a}", tag=tag)
@@ -213,7 +217,7 @@ def tile_picked_sub_mlp_gelu_sub_e_kernel(
                 start=True,
                 stop=True,
             )
-            copy = nc.scalar.copy if b - a == SLICE else nc.vector.tensor_copy
+            copy = nc.scalar.copy if b - a <= SLICE else nc.vector.tensor_copy
             copy(y[:, a:b], y_part[:])
 
         terms = []

@@ -217,7 +217,7 @@ def tile_picked_sub_mlp_gelu_sub_e_kernel(
                 start=True,
                 stop=True,
             )
-            copy = nc.scalar.copy if b - a <= SLICE else nc.vector.tensor_copy
+            copy = nc.vector.tensor_copy if a == 0 else nc.scalar.copy
             copy(y[:, a:b], y_part[:])
 
         terms = []
@@ -226,7 +226,7 @@ def tile_picked_sub_mlp_gelu_sub_e_kernel(
             terms.append(term)
         part = keep.tile([P, V], F32, name="part")
         total = keep.tile([P, V], F32, name="total")
-        halves = (slice(0, V // 2), slice(V // 2, V))
+        halves = (slice(0, 2 * V // 3), slice(2 * V // 3, V))
 
         def fetch(d, cols):
             nc.vector.tensor_tensor(

@@ -22,9 +22,9 @@ PASSES = K // K_PASS
 SLICE = 128
 SLICES = S // SLICE
 THIRD = S // 3
-M_SPLIT = 84
+M_EARLY = 40
+M_LATE = 44
 M_SPLIT0 = 40
-WARM = 4
 
 
 def tile_picked_sub_mlp_gelu_sub_e_kernel(
@@ -58,10 +58,10 @@ def tile_picked_sub_mlp_gelu_sub_e_kernel(
         nc.sync.dma_start(w1_raw0[:], w1_rows(0))
         for t in range(PACK):
             planes.append(load_plane(1, t))
-        w1_raw1a = keep.tile([P, 2, H], F32, name="w1_raw1a")
-        nc.sync.dma_start(w1_raw1a[:], w1_rows(1)[:, 0:2, :])
-        w1_raw1b = keep.tile([P, 2, H], F32, align_bytes=64, name="w1_raw1b", tag="late")
-        nc.sync.dma_start(w1_raw1b[:], w1_rows(1)[:, 2:4, :])
+        w1_raw1a = keep.tile([P, PACK, H // 2], F32, name="w1_raw1a")
+        nc.sync.dma_start(w1_raw1a[:], w1_rows(1)[:, :, 0 : H // 2])
+        w1_raw1b = keep.tile([P, PACK, H // 2], F32, align_bytes=64, name="w1_raw1b", tag="late")
+        nc.sync.dma_start(w1_raw1b[:], w1_rows(1)[:, :, H // 2 : H])
         w2_raw = keep.tile([P, PACK, N], F32, name="w2_raw")
         nc.sync.dma_start(w2_raw[:], w2.rearrange("(p j) n -> p j n", j=PACK))
         places = []
@@ -113,55 +113,22 @@ def tile_picked_sub_mlp_gelu_sub_e_kernel(
             cols = slice(c * THIRD, (c + 1) * THIRD)
             quantise(x_codes[0][:, cols], x_scales[0][:, cols], xg0[:, cols, :].rearrange("p n t -> p (n t)"))
         nc.vector.tensor_copy(grouped0[:, 0:M_SPLIT0], raw0[:, 0:M_SPLIT0])
-        w1_codes0 = keep.tile([P, H], U32, align_bytes=64, name="w1_codes0")
-        w1_scales0 = keep.tile([P, H], U8, align_bytes=64, name="w1_scales0")
-        quantise(w1_codes0[:], w1_scales0[:], w1_grouped0[:].rearrange("p t m j -> p (t m j)"))
-
-        picked1 = keep.tile([P, PACK, S], F32, name="picked1")
-        xg1a = keep.tile([P, THIRD, PACK], BF16, align_bytes=64, name="xg1a")
-        nc.vector.tensor_copy(picked1[:, 0, :], planes[4][:].indirect(offsets[:]))
-        nc.vector.tensor_copy(picked1[:, 1, :], planes[5][:].indirect(offsets[:]))
-        nc.scalar.copy(xg1a[:, :, 0:2], picked1[:, 0:2, 0:THIRD].rearrange("p t n -> p n t"))
-        for t in (2, 3):
-            nc.vector.tensor_copy(xg1a[:, :, t], planes[4 + t][:].indirect(entries(0, THIRD)))
-            nc.vector.tensor_copy(picked1[:, t, THIRD:S], planes[4 + t][:].indirect(entries(THIRD, S)))
-        quantise(x_codes[1][:, 0:THIRD], x_scales[1][:, 0:THIRD], xg1a[:].rearrange("p n t -> p (n t)"))
-
-        w1_codes1 = keep.tile([P, H], U32, align_bytes=64, name="w1_codes1")
+        w1_planes0 = keep.tile([P, P], U8, align_bytes=64, name="w1_planes0")
         w1_scales1 = keep.tile([P, H], U8, align_bytes=64, name="w1_scales1")
-        w1_grouped1 = keep.tile([P, PACK, P, PACK], BF16, align_bytes=64, name="w1_grouped1")
-        grouped1 = w1_grouped1[:].rearrange("p t m j -> p m j t")
-        raw1a = w1_raw1a[:].rearrange("p j (m t) -> p m j t", t=PACK)
-        raw1b = w1_raw1b[:].rearrange("p j (m t) -> p m j t", t=PACK)
-        gpsimd_copy(
-            grouped1[:, M_SPLIT:P, 0:2, :].rearrange("p m j t -> p m t j"),
-            raw1a[:, M_SPLIT:P].rearrange("p m j t -> p m t j"),
+        w1_scales = (
+            [w1_planes0[PACK * t : P, :] for t in range(PACK)],
+            [w1_scales1[:, t * P : (t + 1) * P] for t in range(PACK)],
         )
-        nc.scalar.copy(grouped1[:, 0:M_SPLIT, 0:2, :], raw1a[:, 0:M_SPLIT])
-        for a, b in ((0, 2), (2, 4)):
-            nc.vector.tensor_copy(grouped1[:, 0:M_SPLIT, 2:4, a:b], raw1b[:, 0:M_SPLIT, :, a:b])
-            nc.scalar.copy(grouped1[:, M_SPLIT:P, 2:4, a:b], raw1b[:, M_SPLIT:P, :, a:b])
-        for a, b in ((0, 2), (2, 3), (3, 4)):
-            quantise(
-                w1_codes1[:, P * a : P * b],
-                w1_scales1[:, P * a : P * b],
-                w1_grouped1[:, a:b].rearrange("p t m j -> p (t m j)"),
-            )
-        xg1bc = keep.tile([P, 2 * THIRD, PACK], BF16, align_bytes=64, name="xg1bc", tag="late")
-        weave_all(nc.scalar.copy, xg1bc[:, 0:THIRD, :], picked1[:, :, THIRD : 2 * THIRD])
-        weave_all(nc.vector.tensor_copy, xg1bc[:, THIRD : 2 * THIRD, :], picked1[:, :, 2 * THIRD : S])
-        for c in (1, 2):
-            cols = slice(c * THIRD, (c + 1) * THIRD)
-            src = xg1bc[:, (c - 1) * THIRD : c * THIRD, :]
-            quantise(x_codes[1][:, cols], x_scales[1][:, cols], src.rearrange("p n t -> p (n t)"))
-        w2_grouped = keep.tile([P, N, PACK], BF16, align_bytes=64, name="w2_grouped")
-        w2_codes = keep.tile([P, N], U32, align_bytes=64, name="w2_codes")
-        w2_scales = keep.tile([P, N], U8, align_bytes=64, name="w2_scales")
-        weave_all(nc.vector.tensor_copy, w2_grouped[:], w2_raw[:])
-        quantise(w2_codes[:], w2_scales[:], w2_grouped[:].rearrange("p n j -> p (n j)"))
+        w1_codes = ([], [])
 
-        w1_codes = (w1_codes0, w1_codes1)
-        w1_scales = (w1_scales0, w1_scales1)
+        def quantise_w1_tile(t, tag):
+            codes = keep.tile([P, P], U32, align_bytes=64, name=f"w1_codes0{t}", tag=tag)
+            quantise(codes[:], w1_scales[0][t], w1_grouped0[:, t].rearrange("p m j -> p (m j)"))
+            w1_codes[0].append(codes[:])
+
+        for t in range(PACK - 1):
+            quantise_w1_tile(t, f"w1_codes0{t}")
+
         acc = []
         for i in range(SLICES):
             acc.append(banks.tile([P, PACK, SLICE], F32, name=f"acc{i}", tag=f"acc{i}"))
@@ -171,27 +138,65 @@ def tile_picked_sub_mlp_gelu_sub_e_kernel(
             for t in range(PACK):
                 nc.tensor.matmul_mx(
                     out=acc[i][:, t, :],
-                    lhsT=w1_codes[s][:, t * P : (t + 1) * P].bitcast(FP8X4),
-                    lhsT_scale=w1_scales[s][:, t * P : (t + 1) * P],
+                    lhsT=w1_codes[s][t].bitcast(FP8X4),
+                    lhsT_scale=w1_scales[s][t],
                     rhs=x_codes[s][:, cols].bitcast(FP8X4),
                     rhs_scale=x_scales[s][:, cols],
                     start=(s == 0 and t == 0),
                     stop=(s == PASSES - 1 and t == PACK - 1),
                 )
 
+        picked1 = keep.tile([P, PACK, S], F32, name="picked1")
+        xg1a = keep.tile([P, THIRD, PACK], BF16, align_bytes=64, name="xg1a")
+        nc.vector.tensor_copy(picked1[:, 0, :], planes[4][:].indirect(offsets[:]))
+        nc.vector.tensor_copy(picked1[:, 1, :], planes[5][:].indirect(offsets[:]))
+        nc.scalar.copy(xg1a[:, :, 0:2], picked1[:, 0:2, 0:THIRD].rearrange("p t n -> p n t"))
+        for t in (2, 3):
+            nc.vector.tensor_copy(xg1a[:, :, t], planes[4 + t][:].indirect(entries(0, THIRD)))
+            nc.vector.tensor_copy(picked1[:, t, THIRD:S], planes[4 + t][:].indirect(entries(THIRD, S)))
+            if t == 2:
+                quantise_w1_tile(PACK - 1, "plane12")
         for i in range(SLICES):
             layer1(i, 0)
-        warm = banks.tile([P, THIRD], F32, name="warm", tag="y1")
-        for r in range(WARM):
-            nc.tensor.matmul_mx(
-                out=warm[:],
-                lhsT=w1_codes0[:, 0:P].bitcast(FP8X4),
-                lhsT_scale=w1_scales0[:, 0:P],
-                rhs=x_codes[1][:, 0:THIRD].bitcast(FP8X4),
-                rhs_scale=x_scales[1][:, 0:THIRD],
-                start=True,
-                stop=True,
+        quantise(x_codes[1][:, 0:THIRD], x_scales[1][:, 0:THIRD], xg1a[:].rearrange("p n t -> p (n t)"))
+
+        w1_codes1 = keep.tile([P, H], U32, align_bytes=64, name="w1_codes1")
+        w1_codes[1].extend([w1_codes1[:, t * P : (t + 1) * P] for t in range(PACK)])
+        w1_grouped1 = keep.tile([P, PACK, P, PACK], BF16, align_bytes=64, name="w1_grouped1", tag="w1_grouped1")
+        grouped1 = w1_grouped1[:].rearrange("p t m j -> p m j t")
+        raw1a = w1_raw1a[:].rearrange("p j (m t) -> p m j t", t=PACK)
+        raw1b = w1_raw1b[:].rearrange("p j (m t) -> p m j t", t=PACK)
+        half = P // 2
+        gpsimd_copy(
+            grouped1[:, M_EARLY:half].rearrange("p m j t -> p m t j"),
+            raw1a[:, M_EARLY:half].rearrange("p m j t -> p m t j"),
+        )
+        nc.scalar.copy(grouped1[:, 0:M_EARLY], raw1a[:, 0:M_EARLY])
+        for a, b in ((0, 2), (2, 4)):
+            nc.vector.tensor_copy(grouped1[:, half : half + M_LATE, :, a:b], raw1b[:, 0:M_LATE, :, a:b])
+            nc.scalar.copy(grouped1[:, half + M_LATE : P, :, a:b], raw1b[:, M_LATE:half, :, a:b])
+        for a, b in ((0, 2), (2, 3), (3, 4)):
+            quantise(
+                w1_codes1[:, P * a : P * b],
+                w1_scales1[:, P * a : P * b],
+                w1_grouped1[:, a:b].rearrange("p t m j -> p (t m j)"),
             )
+        xg1b = keep.tile([P, SLICE, PACK], BF16, align_bytes=64, name="xg1b", tag="late")
+        xg1c = keep.tile([P, 3 * SLICE, PACK], BF16, align_bytes=64, name="xg1c", tag="w1_grouped1")
+        weave_all(nc.scalar.copy, xg1b[:], picked1[:, :, 2 * SLICE : 3 * SLICE])
+        weave_all(nc.vector.tensor_copy, xg1c[:, 0:SLICE, :], picked1[:, :, 3 * SLICE : 4 * SLICE])
+        pieces = ((2, 3, xg1b[:]), (3, 4, xg1c[:, 0:SLICE, :]), (4, 6, xg1c[:, SLICE : 3 * SLICE, :]))
+        for a, b, src in pieces:
+            cols = slice(a * SLICE, b * SLICE)
+            quantise(x_codes[1][:, cols], x_scales[1][:, cols], src.rearrange("p n t -> p (n t)"))
+            if a == 2:
+                weave_all(nc.vector.tensor_copy, xg1c[:, SLICE : 3 * SLICE, :], picked1[:, :, 4 * SLICE : S])
+        w2_grouped = keep.tile([P, N, PACK], BF16, align_bytes=64, name="w2_grouped")
+        w2_codes = keep.tile([P, N], U32, align_bytes=64, name="w2_codes")
+        w2_scales = keep.tile([P, N], U8, align_bytes=64, name="w2_scales")
+        weave_all(nc.vector.tensor_copy, w2_grouped[:], w2_raw[:])
+        quantise(w2_codes[:], w2_scales[:], w2_grouped[:].rearrange("p n j -> p (n j)"))
+
         h = keep.tile([P, S, PACK], BF16, align_bytes=64, name="h")
         for i in range(SLICES):
             layer1(i, 1)

@@ -1,6 +1,7 @@
 from contextlib import ExitStack
 
 import concourse.mybir as mybir
+from concourse.masks import make_identity
 
 K, T, D, S, V, H, N = 1024, 2048, 3, 768, 384, 512, 128
 FLOPS = 2 * K * H * S + 2 * H * N * S
@@ -39,6 +40,9 @@ def tile_picked_sub_mlp_gelu_sub_e_kernel(
         nc.vector.memset(dummy[:], 0.0)
         dummy_out = keep.tile([P, 1], F32, name="dummy_out")
         nc.scalar.activation(dummy_out[:], dummy[:], GELU)
+
+        ident = keep.tile([P, P], F32, name="ident")
+        make_identity(nc, ident[:])
 
         def load_plane(s, t):
             rows = xT[s * K_PASS : (s + 1) * K_PASS, :].rearrange("(p t) c -> p t c", t=PACK)
@@ -229,23 +233,39 @@ def tile_picked_sub_mlp_gelu_sub_e_kernel(
         for d in range(D):
             term = keep.tile([P, V], F32, name=f"term{d}")
             terms.append(term)
-        part = keep.tile([P, V], F32, name="part")
-        total = keep.tile([P, V], F32, name="total")
-        halves = (slice(0, 2 * V // 3), slice(2 * V // 3, V))
+        first, second, third = (slice(i * P, (i + 1) * P) for i in range(3))
 
-        def fetch(d, cols):
+        def fetch(d, a, b):
             nc.vector.tensor_tensor(
-                terms[d][:, cols],
-                y[:].indirect(places[d][:, cols.start // 16 : cols.stop // 16]),
-                gates[:, d, cols],
-                MULT,
+                terms[d][:, a:b], y[:].indirect(places[d][:, a // 16 : b // 16]), gates[:, d, a:b], MULT
             )
 
-        fetch(0, slice(0, V))
-        fetch(1, slice(0, V))
-        fetch(2, halves[0])
-        nc.vector.tensor_add(part[:], terms[0][:], terms[1][:])
-        fetch(2, halves[1])
-        for cols in halves:
-            nc.vector.tensor_add(total[:, cols], part[:, cols], terms[2][:, cols])
-            nc.sync.dma_start(out[:, cols], total[:, cols])
+        def turned_sum(cols, count, tags):
+            turned = banks.tile([P, P], F32, name=f"turned{cols.start}", tag=tags[0])
+            for d in range(count):
+                nc.tensor.matmul(
+                    turned[:], terms[d][:, cols], ident[:], start=(d == 0), stop=(d == count - 1), is_transpose=True
+                )
+            held = keep.tile([P, P], F32, name=f"held{cols.start}")
+            nc.scalar.copy(held[:], turned[:])
+            back = banks.tile([P, P], F32, name=f"back{cols.start}", tag=tags[1])
+            nc.tensor.transpose(back[:], held[:], ident[:])
+            return back
+
+        for d in range(D):
+            fetch(d, 0, P)
+        back_first = turned_sum(first, 3, ("acc4", "y0"))
+        total_first = keep.tile([P, P], F32, name="total_first")
+        nc.scalar.copy(total_first[:], back_first[:])
+        nc.sync.dma_start(out[:, first], total_first[:])
+        for d in range(D):
+            fetch(d, P, V)
+        part = keep.tile([P, 2 * P], F32, name="part")
+        total = keep.tile([P, 2 * P], F32, name="total")
+        for cols in (second, third):
+            rest = slice(cols.start - P, cols.stop - P)
+            nc.vector.tensor_add(part[:, rest], terms[0][:, cols], terms[1][:, cols])
+        for cols in (second, third):
+            rest = slice(cols.start - P, cols.stop - P)
+            nc.vector.tensor_add(total[:, rest], part[:, rest], terms[2][:, cols])
+        nc.sync.dma_start(out[:, P:V], total[:])

@@ -157,7 +157,8 @@ def tile_picked_sub_mlp_gelu_sub_e_kernel(
         nc.scalar.copy(xg1a[:, :, 0:2], picked1[:, 0:2, 0:THIRD].rearrange("p t n -> p n t"))
         for t in (2, 3):
             nc.vector.tensor_copy(xg1a[:, :, t], planes[4 + t][:].indirect(entries(0, THIRD)))
-            nc.vector.tensor_copy(picked1[:, t, THIRD:S], planes[4 + t][:].indirect(entries(THIRD, S)))
+            stop = S if t == 2 else S - SLICE
+            nc.vector.tensor_copy(picked1[:, t, THIRD:stop], planes[4 + t][:].indirect(entries(THIRD, stop)))
             if t == 2:
                 quantise_w1_tile(PACK - 1, "plane12")
         for i in range(SLICES):
@@ -176,29 +177,45 @@ def tile_picked_sub_mlp_gelu_sub_e_kernel(
             raw1a[:, M_EARLY:half].rearrange("p m j t -> p m t j"),
         )
         nc.scalar.copy(grouped1[:, 0:M_EARLY], raw1a[:, 0:M_EARLY])
+
+        def quantise_w1_half(t, m0):
+            cols = slice(P * t + m0, P * t + m0 + half)
+            quantise(
+                w1_codes1[:, cols],
+                w1_scales1[:, cols],
+                w1_grouped1[:, t, m0 : m0 + half, :].rearrange("p m j -> p (m j)"),
+            )
+
+        for t in range(PACK):
+            quantise_w1_half(t, 0)
         for a, b in ((0, 2), (2, 4)):
             nc.vector.tensor_copy(grouped1[:, half : half + M_LATE, :, a:b], raw1b[:, 0:M_LATE, :, a:b])
             nc.scalar.copy(grouped1[:, half + M_LATE : P, :, a:b], raw1b[:, M_LATE:half, :, a:b])
-        for a, b in ((0, 2), (2, 3), (3, 4)):
-            quantise(
-                w1_codes1[:, P * a : P * b],
-                w1_scales1[:, P * a : P * b],
-                w1_grouped1[:, a:b].rearrange("p t m j -> p (t m j)"),
-            )
+        for t in range(PACK):
+            quantise_w1_half(t, half)
         xg1b = keep.tile([P, SLICE, PACK], BF16, align_bytes=64, name="xg1b", tag="late")
-        xg1c = keep.tile([P, 3 * SLICE, PACK], BF16, align_bytes=64, name="xg1c", tag="w1_grouped1")
+        xg1c = keep.tile([P, 3 * SLICE + SLICE // PACK, PACK], BF16, align_bytes=64, name="xg1c", tag="w1_grouped1")
         weave_all(nc.scalar.copy, xg1b[:], picked1[:, :, 2 * SLICE : 3 * SLICE])
         weave_all(nc.vector.tensor_copy, xg1c[:, 0:SLICE, :], picked1[:, :, 3 * SLICE : 4 * SLICE])
-        pieces = ((2, 3, xg1b[:]), (3, 4, xg1c[:, 0:SLICE, :]), (4, 6, xg1c[:, SLICE : 3 * SLICE, :]))
-        for a, b, src in pieces:
-            cols = slice(a * SLICE, b * SLICE)
+
+        def quantise_x1(i, src):
+            cols = slice(i * SLICE, (i + 1) * SLICE)
             quantise(x_codes[1][:, cols], x_scales[1][:, cols], src.rearrange("p n t -> p (n t)"))
-            if a == 2:
-                weave_all(nc.vector.tensor_copy, xg1c[:, SLICE : 3 * SLICE, :], picked1[:, :, 4 * SLICE : S])
+
+        quantise_x1(2, xg1b[:])
+        weave_all(nc.vector.tensor_copy, xg1c[:, SLICE : 2 * SLICE, :], picked1[:, :, 4 * SLICE : 5 * SLICE])
+        quantise_x1(3, xg1c[:, 0:SLICE, :])
+        last_row = xg1c[:, 3 * SLICE : 3 * SLICE + SLICE // PACK, :].rearrange("p n t -> p (n t)")
+        nc.vector.tensor_copy(last_row, planes[7][:].indirect(entries(S - SLICE, S)))
+        quantise_x1(4, xg1c[:, SLICE : 2 * SLICE, :])
+        last = xg1c[:, 2 * SLICE : 3 * SLICE, :]
+        nc.vector.tensor_copy(last[:, :, 0:3], picked1[:, 0:3, S - SLICE : S].rearrange("p t n -> p n t"))
+        nc.vector.tensor_copy(last[:, :, 3], last_row)
         w2_grouped = keep.tile([P, N, PACK], BF16, align_bytes=64, name="w2_grouped")
         w2_codes = keep.tile([P, N], U32, align_bytes=64, name="w2_codes")
         w2_scales = keep.tile([P, N], U8, align_bytes=64, name="w2_scales")
         weave_all(nc.vector.tensor_copy, w2_grouped[:], w2_raw[:])
+        quantise_x1(5, last)
         quantise(w2_codes[:], w2_scales[:], w2_grouped[:].rearrange("p n j -> p (n j)"))
 
         h = keep.tile([P, S, PACK], BF16, align_bytes=64, name="h")
@@ -268,4 +285,5 @@ def tile_picked_sub_mlp_gelu_sub_e_kernel(
         for cols in (second, third):
             rest = slice(cols.start - P, cols.stop - P)
             nc.vector.tensor_add(total[:, rest], part[:, rest], terms[2][:, cols])
-        nc.sync.dma_start(out[:, P:V], total[:])
+            queue = nc.scalar if cols.start == P else nc.sync
+            queue.dma_start(out[:, cols], total[:, rest])

@@ -25,7 +25,7 @@ SLICES = S // SLICE
 THIRD = S // 3
 M_EARLY = 40
 M_LATE = 44
-M_SPLIT0 = 40
+M_SPLIT0 = 64
 
 
 def tile_picked_sub_mlp_gelu_sub_e_kernel(
@@ -44,24 +44,25 @@ def tile_picked_sub_mlp_gelu_sub_e_kernel(
         ident = keep.tile([P, P], F32, name="ident")
         make_identity(nc, ident[:])
 
-        def load_plane(s, t):
+        def load_planes(s, t, count):
             rows = xT[s * K_PASS : (s + 1) * K_PASS, :].rearrange("(p t) c -> p t c", t=PACK)
-            plane = keep.tile([P, T], F32, align_bytes=64, name=f"plane{s}{t}", tag=f"plane{s}{t}")
-            nc.sync.dma_start(plane[:], rows[:, t, :])
-            return plane
+            group = keep.tile([P, count, T], F32, align_bytes=64, name=f"plane{s}{t}", tag=f"plane{s}{t}")
+            nc.sync.dma_start(group[:], rows[:, t : t + count, :])
+            return [group[:, i, :] for i in range(count)]
 
         def w1_rows(s):
             return w1[s * K_PASS : (s + 1) * K_PASS, :].rearrange("(p j) c -> p j c", j=PACK)
 
-        planes = [load_plane(0, 0)]
+        planes = load_planes(0, 0, 2)
         offsets = keep.tile([P, S // 16], U16, name="offsets")
         nc.sync.dma_start(offsets[:], offs)
-        for t in range(1, PACK):
-            planes.append(load_plane(0, t))
-        w1_raw0 = keep.tile([P, PACK, H], F32, name="w1_raw0")
+        for t in (2, 3):
+            planes.extend(load_planes(0, t, 1))
+        planes.extend(load_planes(1, 0, 2))
+        w1_raw0 = keep.tile([P, PACK, H], F32, align_bytes=64, name="w1_raw0", tag="w1_raw0")
         nc.sync.dma_start(w1_raw0[:], w1_rows(0))
-        for t in range(PACK):
-            planes.append(load_plane(1, t))
+        for t in (2, 3):
+            planes.extend(load_planes(1, t, 1))
         w1_raw1a = keep.tile([P, PACK, H // 2], F32, name="w1_raw1a")
         nc.sync.dma_start(w1_raw1a[:], w1_rows(1)[:, :, 0 : H // 2])
         w1_raw1b = keep.tile([P, PACK, H // 2], F32, align_bytes=64, name="w1_raw1b", tag="late")
@@ -92,46 +93,52 @@ def tile_picked_sub_mlp_gelu_sub_e_kernel(
             nc.gpsimd.tensor_scalar(dst, src, 1.0, 0.0, MULT, ADD)
 
         x_codes = []
-        x_scales = []
+        x_scales1 = keep.tile([P, S], U8, align_bytes=64, name="x_scales1")
         for s in range(PASSES):
             x_codes.append(keep.tile([P, S], U32, align_bytes=64, name=f"x_codes{s}"))
-            x_scales.append(keep.tile([P, S], U8, align_bytes=64, name=f"x_scales{s}"))
 
         xg0 = keep.tile([P, S, PACK], BF16, align_bytes=64, name="xg0")
         picked01 = keep.tile([P, 2, S], F32, name="picked01")
         picked23 = keep.tile([P, 2, S], F32, name="picked23")
         for t in range(2):
-            nc.vector.tensor_copy(picked01[:, t, :], planes[t][:].indirect(offsets[:]))
+            nc.vector.tensor_copy(picked01[:, t, :], planes[t].indirect(offsets[:]))
         nc.scalar.copy(xg0[:, :, 0:2], picked01[:].rearrange("p t n -> p n t"))
-        for t in range(2):
-            nc.vector.tensor_copy(picked23[:, t, :], planes[2 + t][:].indirect(offsets[:]))
+        nc.vector.tensor_copy(picked23[:, 0, :], planes[2].indirect(offsets[:]))
         for c in range(3):
             cols = slice(c * THIRD, (c + 1) * THIRD)
-            copy = nc.vector.tensor_copy if c < 2 else nc.scalar.copy
+            nc.vector.tensor_copy(picked23[:, 1, cols], planes[3].indirect(entries(cols.start, cols.stop)))
+            copy = gpsimd_copy if c == 1 else nc.scalar.copy
             copy(xg0[:, cols, 2:4], picked23[:, :, cols].rearrange("p t n -> p n t"))
+        x_planes0 = keep.tile([P, THIRD], U8, align_bytes=64, name="x_planes0")
+        across = slice(SLICE // 2, SLICE // 2 + SLICE)
+        x_scales0 = keep.tile([P, THIRD], U8, align_bytes=64, name="x_scales0")
+        for cols, scales in (
+            (slice(0, THIRD), x_planes0[:]),
+            (slice(THIRD, THIRD + SLICE), x_planes0[PACK:P, across]),
+            (slice(2 * THIRD, S), x_scales0[:]),
+        ):
+            quantise(x_codes[0][:, cols], scales, xg0[:, cols, :].rearrange("p n t -> p (n t)"))
+        picked1 = keep.tile([P, PACK, S], F32, name="picked1")
+        nc.vector.tensor_copy(picked1[:, 0, :], planes[4].indirect(offsets[:]))
+        nc.vector.tensor_copy(picked1[:, 1, :], planes[5].indirect(offsets[:]))
         w1_grouped0 = keep.tile([P, PACK, P, PACK], BF16, align_bytes=64, name="w1_grouped0")
         raw0 = w1_raw0[:].rearrange("p j (m t) -> p m j t", t=PACK)
         grouped0 = w1_grouped0[:].rearrange("p t m j -> p m j t")
         nc.scalar.copy(grouped0[:, M_SPLIT0:P], raw0[:, M_SPLIT0:P])
-        for c in range(3):
-            cols = slice(c * THIRD, (c + 1) * THIRD)
-            quantise(x_codes[0][:, cols], x_scales[0][:, cols], xg0[:, cols, :].rearrange("p n t -> p (n t)"))
-        nc.vector.tensor_copy(grouped0[:, 0:M_SPLIT0], raw0[:, 0:M_SPLIT0])
-        w1_planes0 = keep.tile([P, P], U8, align_bytes=64, name="w1_planes0")
+        gpsimd_copy(
+            grouped0[:, 0:M_SPLIT0].rearrange("p m j t -> p m t j"),
+            raw0[:, 0:M_SPLIT0].rearrange("p m j t -> p m t j"),
+        )
+        w1_scales0 = keep.tile([P, H], U8, align_bytes=64, name="w1_scales0")
         w1_scales1 = keep.tile([P, H], U8, align_bytes=64, name="w1_scales1")
         w1_scales = (
-            [w1_planes0[PACK * t : P, :] for t in range(PACK)],
+            [w1_scales0[:, t * P : (t + 1) * P] for t in range(PACK)],
             [w1_scales1[:, t * P : (t + 1) * P] for t in range(PACK)],
         )
         w1_codes = ([], [])
-
-        def quantise_w1_tile(t, tag):
-            codes = keep.tile([P, P], U32, align_bytes=64, name=f"w1_codes0{t}", tag=tag)
-            quantise(codes[:], w1_scales[0][t], w1_grouped0[:, t].rearrange("p m j -> p (m j)"))
-            w1_codes[0].append(codes[:])
-
-        for t in range(PACK - 1):
-            quantise_w1_tile(t, f"w1_codes0{t}")
+        w1_codes0 = keep.tile([P, H], U32, align_bytes=64, name="w1_codes0")
+        w1_codes[0].extend([w1_codes0[:, t * P : (t + 1) * P] for t in range(PACK)])
+        quantise(w1_codes0[:], w1_scales0[:], w1_grouped0[:].rearrange("p t m j -> p (t m j)"))
 
         acc = []
         for i in range(SLICES):
@@ -139,31 +146,43 @@ def tile_picked_sub_mlp_gelu_sub_e_kernel(
 
         def layer1(i, s):
             cols = slice(i * SLICE, (i + 1) * SLICE)
+            codes = x_codes[s][:, cols]
+            scales = x_scales1[:, cols]
+            if s == 0 and i < 2:
+                scales = x_planes0[:, cols]
+            if s == 0 and i in (2, 3):
+                scales = x_planes0[PACK * (i - 1) : P, across]
+            if s == 0 and i == 3:
+                codes = x_codes_late[:]
+            if s == 0 and i > 3:
+                scales = x_scales0[:, cols.start - 2 * THIRD : cols.stop - 2 * THIRD]
             for t in range(PACK):
                 nc.tensor.matmul_mx(
                     out=acc[i][:, t, :],
                     lhsT=w1_codes[s][t].bitcast(FP8X4),
                     lhsT_scale=w1_scales[s][t],
-                    rhs=x_codes[s][:, cols].bitcast(FP8X4),
-                    rhs_scale=x_scales[s][:, cols],
+                    rhs=codes.bitcast(FP8X4),
+                    rhs_scale=scales,
                     start=(s == 0 and t == 0),
                     stop=(s == PASSES - 1 and t == PACK - 1),
                 )
 
-        picked1 = keep.tile([P, PACK, S], F32, name="picked1")
-        xg1a = keep.tile([P, THIRD, PACK], BF16, align_bytes=64, name="xg1a")
-        nc.vector.tensor_copy(picked1[:, 0, :], planes[4][:].indirect(offsets[:]))
-        nc.vector.tensor_copy(picked1[:, 1, :], planes[5][:].indirect(offsets[:]))
+        xg1a = keep.tile([P, THIRD, PACK], BF16, align_bytes=64, name="xg1a", tag="w1_raw0")
         nc.scalar.copy(xg1a[:, :, 0:2], picked1[:, 0:2, 0:THIRD].rearrange("p t n -> p n t"))
         for t in (2, 3):
-            nc.vector.tensor_copy(xg1a[:, :, t], planes[4 + t][:].indirect(entries(0, THIRD)))
+            nc.vector.tensor_copy(xg1a[:, :, t], planes[4 + t].indirect(entries(0, THIRD)))
             stop = S if t == 2 else S - SLICE
-            nc.vector.tensor_copy(picked1[:, t, THIRD:stop], planes[4 + t][:].indirect(entries(THIRD, stop)))
+            nc.vector.tensor_copy(picked1[:, t, THIRD:stop], planes[4 + t].indirect(entries(THIRD, stop)))
             if t == 2:
-                quantise_w1_tile(PACK - 1, "plane12")
+                x_codes_late = keep.tile([P, SLICE], U32, align_bytes=64, name="x_codes_late", tag="plane12")
+                quantise(
+                    x_codes_late[:],
+                    x_planes0[PACK * 2 : P, across],
+                    xg0[:, 3 * SLICE : 4 * SLICE, :].rearrange("p n t -> p (n t)"),
+                )
         for i in range(SLICES):
             layer1(i, 0)
-        quantise(x_codes[1][:, 0:THIRD], x_scales[1][:, 0:THIRD], xg1a[:].rearrange("p n t -> p (n t)"))
+        quantise(x_codes[1][:, 0:THIRD], x_scales1[:, 0:THIRD], xg1a[:].rearrange("p n t -> p (n t)"))
 
         w1_codes1 = keep.tile([P, H], U32, align_bytes=64, name="w1_codes1")
         w1_codes[1].extend([w1_codes1[:, t * P : (t + 1) * P] for t in range(PACK)])
@@ -200,13 +219,13 @@ def tile_picked_sub_mlp_gelu_sub_e_kernel(
 
         def quantise_x1(i, src):
             cols = slice(i * SLICE, (i + 1) * SLICE)
-            quantise(x_codes[1][:, cols], x_scales[1][:, cols], src.rearrange("p n t -> p (n t)"))
+            quantise(x_codes[1][:, cols], x_scales1[:, cols], src.rearrange("p n t -> p (n t)"))
 
         quantise_x1(2, xg1b[:])
         weave_all(nc.vector.tensor_copy, xg1c[:, SLICE : 2 * SLICE, :], picked1[:, :, 4 * SLICE : 5 * SLICE])
         quantise_x1(3, xg1c[:, 0:SLICE, :])
         last_row = xg1c[:, 3 * SLICE : 3 * SLICE + SLICE // PACK, :].rearrange("p n t -> p (n t)")
-        nc.vector.tensor_copy(last_row, planes[7][:].indirect(entries(S - SLICE, S)))
+        nc.vector.tensor_copy(last_row, planes[7].indirect(entries(S - SLICE, S)))
         quantise_x1(4, xg1c[:, SLICE : 2 * SLICE, :])
         last = xg1c[:, 2 * SLICE : 3 * SLICE, :]
         nc.vector.tensor_copy(last[:, :, 0:3], picked1[:, 0:3, S - SLICE : S].rearrange("p t n -> p n t"))
@@ -285,5 +304,4 @@ def tile_picked_sub_mlp_gelu_sub_e_kernel(
         for cols in (second, third):
             rest = slice(cols.start - P, cols.stop - P)
             nc.vector.tensor_add(total[:, rest], part[:, rest], terms[2][:, cols])
-            queue = nc.scalar if cols.start == P else nc.sync
-            queue.dma_start(out[:, cols], total[:, rest])
+        nc.sync.dma_start(out[:, P:V], total[:])

@@ -191,11 +191,12 @@ def tile_picked_sub_mlp_gelu_sub_e_kernel(
         raw1a = w1_raw1a[:].rearrange("p j (m t) -> p m j t", t=PACK)
         raw1b = w1_raw1b[:].rearrange("p j (m t) -> p m j t", t=PACK)
         half = P // 2
-        gpsimd_copy(
-            grouped1[:, M_EARLY:half].rearrange("p m j t -> p m t j"),
-            raw1a[:, M_EARLY:half].rearrange("p m j t -> p m t j"),
-        )
-        nc.scalar.copy(grouped1[:, 0:M_EARLY], raw1a[:, 0:M_EARLY])
+        for a, b in ((0, 2), (2, 4)):
+            gpsimd_copy(
+                grouped1[:, M_EARLY:half, :, a:b].rearrange("p m j t -> p m t j"),
+                raw1a[:, M_EARLY:half, :, a:b].rearrange("p m j t -> p m t j"),
+            )
+            nc.scalar.copy(grouped1[:, 0:M_EARLY, :, a:b], raw1a[:, 0:M_EARLY, :, a:b])
 
         def quantise_w1_half(t, m0):
             cols = slice(P * t + m0, P * t + m0 + half)
@@ -291,17 +292,15 @@ def tile_picked_sub_mlp_gelu_sub_e_kernel(
         for d in range(D):
             fetch(d, 0, P)
         back_first = turned_sum(first, 3, ("acc4", "y0"))
-        total_first = keep.tile([P, P], F32, name="total_first")
-        nc.scalar.copy(total_first[:], back_first[:])
-        nc.sync.dma_start(out[:, first], total_first[:])
+        total = keep.tile([P, V], F32, name="total")
+        nc.scalar.copy(total[:, first], back_first[:])
         for d in range(D):
             fetch(d, P, V)
         part = keep.tile([P, 2 * P], F32, name="part")
-        total = keep.tile([P, 2 * P], F32, name="total")
         for cols in (second, third):
             rest = slice(cols.start - P, cols.stop - P)
             nc.vector.tensor_add(part[:, rest], terms[0][:, cols], terms[1][:, cols])
         for cols in (second, third):
             rest = slice(cols.start - P, cols.stop - P)
-            nc.vector.tensor_add(total[:, rest], part[:, rest], terms[2][:, cols])
-        nc.sync.dma_start(out[:, P:V], total[:])
+            nc.vector.tensor_add(total[:, cols], part[:, rest], terms[2][:, cols])
+        nc.sync.dma_start(out, total[:])

@@ -244,7 +244,7 @@ def tile_picked_sub_mlp_gelu_sub_e_kernel(
             pieces = ((0, SLICE),) if i < SLICES - 1 else ((0, SLICE // 2), (SLICE // 2, SLICE))
             for a, b in pieces:
                 nc.scalar.activation(
-                    h[:, i * SLICE + a : i * SLICE + b, :], acc[i][:, :, a:b].rearrange("p t n -> p n t"), GELU, bias=dummy_out[:]
+                    h[:, i * SLICE + a : i * SLICE + b, :], acc[i][:, :, a:b].rearrange("p t n -> p n t"), GELU, bias=dummy_out[:] if i == 0 else 0.0
                 )
 
         h_codes = keep.tile([P, S], U32, align_bytes=64, name="h_codes")

@@ -1,7 +1,6 @@
 from contextlib import ExitStack
 
 import concourse.mybir as mybir
-from concourse.masks import make_identity
 
 K, T, D, S, V, H, N = 1024, 2048, 3, 768, 384, 512, 128
 FLOPS = 2 * K * H * S + 2 * H * N * S
@@ -14,6 +13,7 @@ U8 = mybir.dt.uint8
 FP8X4 = mybir.dt.float8_e4m3fn_x4
 MULT = mybir.AluOpType.mult
 ADD = mybir.AluOpType.add
+COPY = mybir.ActivationFunctionType.Copy
 GELU = mybir.ActivationFunctionType.Gelu_apprx_tanh
 
 P = 128
@@ -40,9 +40,6 @@ def tile_picked_sub_mlp_gelu_sub_e_kernel(
         nc.vector.memset(dummy[:], 0.0)
         dummy_out = keep.tile([P, 1], F32, name="dummy_out")
         nc.scalar.activation(dummy_out[:], dummy[:], GELU)
-
-        ident = keep.tile([P, P], F32, name="ident")
-        make_identity(nc, ident[:])
 
         def load_planes(s, t, count):
             rows = xT[s * K_PASS : (s + 1) * K_PASS, :].rearrange("(p t) c -> p t c", t=PACK)
@@ -266,41 +263,36 @@ def tile_picked_sub_mlp_gelu_sub_e_kernel(
             copy = nc.vector.tensor_copy if a == 0 else nc.scalar.copy
             copy(y[:, a:b], y_part[:])
 
-        terms = []
-        for d in range(D):
-            term = keep.tile([P, V], F32, name=f"term{d}")
-            terms.append(term)
-        first, second, third = (slice(i * P, (i + 1) * P) for i in range(3))
-
-        def fetch(d, a, b):
-            nc.vector.tensor_tensor(
-                terms[d][:, a:b], y[:].indirect(places[d][:, a // 16 : b // 16]), gates[:, d, a:b], MULT
-            )
-
-        def turned_sum(cols, count, tags):
-            turned = banks.tile([P, P], F32, name=f"turned{cols.start}", tag=tags[0])
-            for d in range(count):
-                nc.tensor.matmul(
-                    turned[:], terms[d][:, cols], ident[:], start=(d == 0), stop=(d == count - 1), is_transpose=True
-                )
-            held = keep.tile([P, P], F32, name=f"held{cols.start}")
-            nc.scalar.copy(held[:], turned[:])
-            back = banks.tile([P, P], F32, name=f"back{cols.start}", tag=tags[1])
-            nc.tensor.transpose(back[:], held[:], ident[:])
-            return back
-
-        for d in range(D):
-            fetch(d, 0, P)
-        back_first = turned_sum(first, 3, ("acc4", "y0"))
+        blocks = [slice(i * P, (i + 1) * P) for i in range(V // P)]
+        fetched = keep.tile([P, D - 1, V], F32, name="fetched")
+        terms = [keep.tile([P, V], F32, name=f"term{d}") for d in range(D)]
+        pair = keep.tile([P, V], F32, name="pair")
         total = keep.tile([P, V], F32, name="total")
-        nc.scalar.copy(total[:, first], back_first[:])
-        for d in range(D):
-            fetch(d, P, V)
-        part = keep.tile([P, 2 * P], F32, name="part")
-        for cols in (second, third):
-            rest = slice(cols.start - P, cols.stop - P)
-            nc.vector.tensor_add(part[:, rest], terms[0][:, cols], terms[1][:, cols])
-        for cols in (second, third):
-            rest = slice(cols.start - P, cols.stop - P)
-            nc.vector.tensor_add(total[:, cols], part[:, rest], terms[2][:, cols])
+        for cols in blocks:
+            for d in (1, 2):
+                window = y[:].indirect(places[d][:, cols.start // 16 : cols.stop // 16])
+                nc.scalar.activation(fetched[:, d - 1, cols], window, COPY)
+        nc.vector.tensor_tensor(terms[0][:], y[:].indirect(places[0][:]), gates[:, 0, :], MULT)
+
+        def weigh(d, b):
+            nc.vector.tensor_mul(terms[d][:, blocks[b]], fetched[:, d - 1, blocks[b]], gates[:, d, blocks[b]])
+
+        def add_pair(b):
+            nc.vector.tensor_add(pair[:, blocks[b]], terms[0][:, blocks[b]], terms[1][:, blocks[b]])
+
+        def add_third(b):
+            nc.vector.tensor_add(total[:, blocks[b]], pair[:, blocks[b]], terms[2][:, blocks[b]])
+
+        weigh(1, 0)
+        weigh(2, 0)
+        weigh(1, 1)
+        add_pair(0)
+        weigh(2, 1)
+        add_pair(1)
+        weigh(1, 2)
+        add_third(0)
+        weigh(2, 2)
+        add_pair(2)
+        add_third(1)
+        add_third(2)
         nc.sync.dma_start(out, total[:])

@@ -13,8 +13,9 @@ U8 = mybir.dt.uint8
 FP8X4 = mybir.dt.float8_e4m3fn_x4
 MULT = mybir.AluOpType.mult
 ADD = mybir.AluOpType.add
-COPY = mybir.ActivationFunctionType.Copy
 GELU = mybir.ActivationFunctionType.Gelu_apprx_tanh
+COPY = mybir.ActivationFunctionType.Copy
+IDENTITY = mybir.ActivationFunctionType.Identity
 
 P = 128
 PACK = 4
@@ -24,8 +25,7 @@ SLICE = 128
 SLICES = S // SLICE
 THIRD = S // 3
 M_EARLY = 40
-M_LATE = 44
-M_SPLIT0 = 64
+M_LATE = 40
 
 
 def tile_picked_sub_mlp_gelu_sub_e_kernel(
@@ -36,33 +36,32 @@ def tile_picked_sub_mlp_gelu_sub_e_kernel(
         keep = ctx.enter_context(tc.tile_pool(name="keep", bufs=1))
         banks = ctx.enter_context(tc.psum_pool(name="banks", bufs=1))
 
-        dummy = keep.tile([P, 1], F32, name="dummy")
-        nc.vector.memset(dummy[:], 0.0)
-        dummy_out = keep.tile([P, 1], F32, name="dummy_out")
-        nc.scalar.activation(dummy_out[:], dummy[:], GELU)
+        zero = keep.tile([P, 1], F32, name="zero")
+        nc.vector.memset(zero[:], 0.0)
+        gelu_zero = keep.tile([P, 1], F32, name="gelu_zero")
+        nc.scalar.activation(gelu_zero[:], zero[:], GELU)
 
-        def load_planes(s, t, count):
+        def load_rows(s, t, count):
             rows = xT[s * K_PASS : (s + 1) * K_PASS, :].rearrange("(p t) c -> p t c", t=PACK)
-            group = keep.tile([P, count, T], F32, align_bytes=64, name=f"plane{s}{t}", tag=f"plane{s}{t}")
+            group = keep.tile([P, count, T], F32, align_bytes=64, name=f"rows{s}{t}")
             nc.sync.dma_start(group[:], rows[:, t : t + count, :])
             return [group[:, i, :] for i in range(count)]
 
         def w1_rows(s):
             return w1[s * K_PASS : (s + 1) * K_PASS, :].rearrange("(p j) c -> p j c", j=PACK)
 
-        planes = load_planes(0, 0, 2)
+        rows = load_rows(0, 0, 2)
         offsets = keep.tile([P, S // 16], U16, name="offsets")
         nc.sync.dma_start(offsets[:], offs)
-        for t in (2, 3):
-            planes.extend(load_planes(0, t, 1))
-        planes.extend(load_planes(1, 0, 2))
-        w1_raw0 = keep.tile([P, PACK, H], F32, align_bytes=64, name="w1_raw0", tag="w1_raw0")
+        rows.extend(load_rows(0, 2, 2))
+        rows.extend(load_rows(1, 0, 2))
+        rows.extend(load_rows(1, 2, 1))
+        w1_raw0 = keep.tile([P, PACK, H], F32, align_bytes=64, name="w1_raw0")
         nc.sync.dma_start(w1_raw0[:], w1_rows(0))
-        for t in (2, 3):
-            planes.extend(load_planes(1, t, 1))
-        w1_raw1a = keep.tile([P, PACK, H // 2], F32, name="w1_raw1a")
+        rows.extend(load_rows(1, 3, 1))
+        w1_raw1a = keep.tile([P, PACK, H // 2], F32, align_bytes=64, name="w1_raw1a")
         nc.sync.dma_start(w1_raw1a[:], w1_rows(1)[:, :, 0 : H // 2])
-        w1_raw1b = keep.tile([P, PACK, H // 2], F32, align_bytes=64, name="w1_raw1b", tag="late")
+        w1_raw1b = keep.tile([P, PACK, H // 2], F32, align_bytes=64, name="w1_raw1b", tag="last_raw")
         nc.sync.dma_start(w1_raw1b[:], w1_rows(1)[:, :, H // 2 : H])
         w2_raw = keep.tile([P, PACK, N], F32, name="w2_raw")
         nc.sync.dma_start(w2_raw[:], w2.rearrange("(p j) n -> p j n", j=PACK))
@@ -74,11 +73,14 @@ def tile_picked_sub_mlp_gelu_sub_e_kernel(
         gates = keep.tile([P, D, V], F32, name="gates")
         nc.sync.dma_start(gates[:], gate.rearrange("d m v -> m d v"))
 
-        def quantise(codes, scales, grouped):
-            nc.vector.quantize_mx(out=codes.bitcast(FP8X4), scales=scales, in_=grouped)
+        def quantise(codes, scales, woven):
+            nc.vector.quantize_mx(out=codes.bitcast(FP8X4), scales=scales, in_=woven)
 
-        def entries(a, b):
-            return offsets[:, a // 16 : b // 16]
+        def picked_from(row, a, b):
+            return row.indirect(offsets[:, a // 16 : b // 16])
+
+        def scalar_gather(dst, src):
+            nc.scalar.activation(dst, src, COPY)
 
         def weave_all(copy, dst, src):
             copy(
@@ -86,162 +88,125 @@ def tile_picked_sub_mlp_gelu_sub_e_kernel(
                 src.rearrange("p t (c i) -> p c t i", i=4),
             )
 
-        def gpsimd_copy(dst, src):
-            nc.gpsimd.tensor_scalar(dst, src, 1.0, 0.0, MULT, ADD)
+        def flat(woven):
+            return woven.rearrange("p n t -> p (n t)")
 
-        x_codes = []
-        x_scales1 = keep.tile([P, S], U8, align_bytes=64, name="x_scales1")
-        for s in range(PASSES):
-            x_codes.append(keep.tile([P, S], U32, align_bytes=64, name=f"x_codes{s}"))
+        x_codes0 = keep.tile([P, S], U32, align_bytes=64, name="x_codes0")
+        x_scales0 = keep.tile([P, S], U8, align_bytes=64, name="x_scales0")
+        x_woven0 = keep.tile([P, S, PACK], BF16, align_bytes=64, name="x_woven0")
+        picked0 = keep.tile([P, PACK, S], F32, name="picked0")
+        for t in range(PACK):
+            gather = nc.vector.tensor_copy if t % 2 == 0 else scalar_gather
+            gather(picked0[:, t, :], picked_from(rows[t], 0, S))
+        cut = 2 * THIRD
+        weave_all(nc.vector.tensor_copy, x_woven0[:, 0:cut, :], picked0[:, :, 0:cut])
+        nc.scalar.activation(
+            x_woven0[:, cut:S, :], picked0[:, :, cut:S].rearrange("p t n -> p n t"), IDENTITY, bias=gelu_zero[:]
+        )
+        for a, b in ((0, cut), (cut, S)):
+            quantise(x_codes0[:, a:b], x_scales0[:, a:b], flat(x_woven0[:, a:b, :]))
 
-        xg0 = keep.tile([P, S, PACK], BF16, align_bytes=64, name="xg0")
-        picked01 = keep.tile([P, 2, S], F32, name="picked01")
-        picked23 = keep.tile([P, 2, S], F32, name="picked23")
-        for t in range(2):
-            nc.vector.tensor_copy(picked01[:, t, :], planes[t].indirect(offsets[:]))
-        nc.scalar.copy(xg0[:, :, 0:2], picked01[:].rearrange("p t n -> p n t"))
-        nc.vector.tensor_copy(picked23[:, 0, :], planes[2].indirect(offsets[:]))
-        for c in range(3):
-            cols = slice(c * THIRD, (c + 1) * THIRD)
-            nc.vector.tensor_copy(picked23[:, 1, cols], planes[3].indirect(entries(cols.start, cols.stop)))
-            copy = gpsimd_copy if c == 1 else nc.scalar.copy
-            copy(xg0[:, cols, 2:4], picked23[:, :, cols].rearrange("p t n -> p n t"))
-        x_planes0 = keep.tile([P, THIRD], U8, align_bytes=64, name="x_planes0")
-        across = slice(SLICE // 2, SLICE // 2 + SLICE)
-        x_scales0 = keep.tile([P, THIRD], U8, align_bytes=64, name="x_scales0")
-        for cols, scales in (
-            (slice(0, THIRD), x_planes0[:]),
-            (slice(THIRD, THIRD + SLICE), x_planes0[PACK:P, across]),
-            (slice(2 * THIRD, S), x_scales0[:]),
-        ):
-            quantise(x_codes[0][:, cols], scales, xg0[:, cols, :].rearrange("p n t -> p (n t)"))
         picked1 = keep.tile([P, PACK, S], F32, name="picked1")
-        nc.vector.tensor_copy(picked1[:, 0, :], planes[4].indirect(offsets[:]))
-        nc.vector.tensor_copy(picked1[:, 1, :], planes[5].indirect(offsets[:]))
-        w1_grouped0 = keep.tile([P, PACK, P, PACK], BF16, align_bytes=64, name="w1_grouped0")
+        nc.vector.tensor_copy(picked1[:, 0, :], picked_from(rows[4], 0, S))
+        for t in (1, 2):
+            scalar_gather(picked1[:, t, :], picked_from(rows[4 + t], 0, S))
+
+        w1_codes = [keep.tile([P, H], U32, align_bytes=64, name=f"w1_codes{s}") for s in range(PASSES)]
+        w1_scales = [keep.tile([P, H], U8, align_bytes=64, name=f"w1_scales{s}") for s in range(PASSES)]
+        w1_woven0 = keep.tile([P, PACK, P, PACK], BF16, align_bytes=64, name="w1_woven0", tag="early")
         raw0 = w1_raw0[:].rearrange("p j (m t) -> p m j t", t=PACK)
-        grouped0 = w1_grouped0[:].rearrange("p t m j -> p m j t")
-        nc.scalar.copy(grouped0[:, M_SPLIT0:P], raw0[:, M_SPLIT0:P])
-        gpsimd_copy(
-            grouped0[:, 0:M_SPLIT0].rearrange("p m j t -> p m t j"),
-            raw0[:, 0:M_SPLIT0].rearrange("p m j t -> p m t j"),
-        )
-        w1_scales0 = keep.tile([P, H], U8, align_bytes=64, name="w1_scales0")
-        w1_scales1 = keep.tile([P, H], U8, align_bytes=64, name="w1_scales1")
-        w1_scales = (
-            [w1_scales0[:, t * P : (t + 1) * P] for t in range(PACK)],
-            [w1_scales1[:, t * P : (t + 1) * P] for t in range(PACK)],
-        )
-        w1_codes = ([], [])
-        w1_codes0 = keep.tile([P, H], U32, align_bytes=64, name="w1_codes0")
-        w1_codes[0].extend([w1_codes0[:, t * P : (t + 1) * P] for t in range(PACK)])
-        quantise(w1_codes0[:], w1_scales0[:], w1_grouped0[:].rearrange("p t m j -> p (t m j)"))
+        woven0 = w1_woven0[:].rearrange("p t m j -> p m j t")
+        for a in (0, 2):
+            nc.vector.tensor_copy(woven0[:, :, :, a : a + 2], raw0[:, :, :, a : a + 2])
+        for a in (0, 2):
+            cols = slice(a * P, (a + 2) * P)
+            quantise(
+                w1_codes[0][:, cols], w1_scales[0][:, cols], w1_woven0[:, a : a + 2].rearrange("p t m j -> p (t m j)")
+            )
 
-        acc = []
-        for i in range(SLICES):
-            acc.append(banks.tile([P, PACK, SLICE], F32, name=f"acc{i}", tag=f"acc{i}"))
+        acc = [banks.tile([P, PACK, SLICE], F32, name=f"acc{i}", tag=f"acc{i}") for i in range(SLICES)]
 
-        def layer1(i, s):
-            cols = slice(i * SLICE, (i + 1) * SLICE)
-            codes = x_codes[s][:, cols]
-            scales = x_scales1[:, cols]
-            if s == 0 and i < 2:
-                scales = x_planes0[:, cols]
-            if s == 0 and i in (2, 3):
-                scales = x_planes0[PACK * (i - 1) : P, across]
-            if s == 0 and i == 3:
-                codes = x_codes_late[:]
-            if s == 0 and i > 3:
-                scales = x_scales0[:, cols.start - 2 * THIRD : cols.stop - 2 * THIRD]
-            for t in range(PACK):
-                nc.tensor.matmul_mx(
-                    out=acc[i][:, t, :],
-                    lhsT=w1_codes[s][t].bitcast(FP8X4),
-                    lhsT_scale=w1_scales[s][t],
-                    rhs=codes.bitcast(FP8X4),
-                    rhs_scale=scales,
-                    start=(s == 0 and t == 0),
-                    stop=(s == PASSES - 1 and t == PACK - 1),
-                )
+        def layer1(i, s, t, codes, scales):
+            nc.tensor.matmul_mx(
+                out=acc[i][:, t, :],
+                lhsT=w1_codes[s][:, t * P : (t + 1) * P].bitcast(FP8X4),
+                lhsT_scale=w1_scales[s][:, t * P : (t + 1) * P],
+                rhs=codes.bitcast(FP8X4),
+                rhs_scale=scales,
+                start=(s == 0 and t == 0),
+                stop=(s == PASSES - 1 and t == PACK - 1),
+            )
 
-        xg1a = keep.tile([P, THIRD, PACK], BF16, align_bytes=64, name="xg1a", tag="w1_raw0")
-        nc.scalar.copy(xg1a[:, :, 0:2], picked1[:, 0:2, 0:THIRD].rearrange("p t n -> p n t"))
-        for t in (2, 3):
-            nc.vector.tensor_copy(xg1a[:, :, t], planes[4 + t].indirect(entries(0, THIRD)))
-            stop = S if t == 2 else S - SLICE
-            nc.vector.tensor_copy(picked1[:, t, THIRD:stop], planes[4 + t].indirect(entries(THIRD, stop)))
-            if t == 2:
-                x_codes_late = keep.tile([P, SLICE], U32, align_bytes=64, name="x_codes_late", tag="plane12")
-                quantise(
-                    x_codes_late[:],
-                    x_planes0[PACK * 2 : P, across],
-                    xg0[:, 3 * SLICE : 4 * SLICE, :].rearrange("p n t -> p (n t)"),
-                )
-        for i in range(SLICES):
-            layer1(i, 0)
-        quantise(x_codes[1][:, 0:THIRD], x_scales1[:, 0:THIRD], xg1a[:].rearrange("p n t -> p (n t)"))
+        for t in range(PACK):
+            for i in range(SLICES):
+                cols = slice(i * SLICE, (i + 1) * SLICE)
+                layer1(i, 0, t, x_codes0[:, cols], x_scales0[:, cols])
 
-        w1_codes1 = keep.tile([P, H], U32, align_bytes=64, name="w1_codes1")
-        w1_codes[1].extend([w1_codes1[:, t * P : (t + 1) * P] for t in range(PACK)])
-        w1_grouped1 = keep.tile([P, PACK, P, PACK], BF16, align_bytes=64, name="w1_grouped1", tag="w1_grouped1")
-        grouped1 = w1_grouped1[:].rearrange("p t m j -> p m j t")
+        scalar_gather(picked1[:, 3, THIRD:S], picked_from(rows[7], THIRD, S))
+        x_scales1 = keep.tile([P, S], U8, align_bytes=64, name="x_scales1")
+        x_codes1a = keep.tile([P, THIRD], U32, align_bytes=64, name="x_codes1a")
+        x_woven1a = keep.tile([P, THIRD, PACK], BF16, align_bytes=64, name="x_woven1a", tag="early")
+        nc.vector.tensor_copy(x_woven1a[:, :, 0:3], picked1[:, 0:3, 0:THIRD].rearrange("p t n -> p n t"))
+        nc.vector.tensor_copy(x_woven1a[:, :, 3], picked_from(rows[7], 0, THIRD))
+        quantise(x_codes1a[:, 0:SLICE], x_scales1[:, 0:SLICE], flat(x_woven1a[:, 0:SLICE, :]))
+
+        half = P // 2
+        w1_woven1a = keep.tile([P, PACK, half, PACK], BF16, align_bytes=64, name="w1_woven1a")
+        w1_woven1b = keep.tile([P, PACK, half, PACK], BF16, align_bytes=64, name="w1_woven1b", tag="last_woven")
         raw1a = w1_raw1a[:].rearrange("p j (m t) -> p m j t", t=PACK)
         raw1b = w1_raw1b[:].rearrange("p j (m t) -> p m j t", t=PACK)
-        half = P // 2
-        for a, b in ((0, 2), (2, 4)):
-            gpsimd_copy(
-                grouped1[:, M_EARLY:half, :, a:b].rearrange("p m j t -> p m t j"),
-                raw1a[:, M_EARLY:half, :, a:b].rearrange("p m j t -> p m t j"),
-            )
-            nc.scalar.copy(grouped1[:, 0:M_EARLY, :, a:b], raw1a[:, 0:M_EARLY, :, a:b])
+        woven1a = w1_woven1a[:].rearrange("p t m j -> p m j t")
+        woven1b = w1_woven1b[:].rearrange("p t m j -> p m j t")
 
-        def quantise_w1_half(t, m0):
-            cols = slice(P * t + m0, P * t + m0 + half)
-            quantise(
-                w1_codes1[:, cols],
-                w1_scales1[:, cols],
-                w1_grouped1[:, t, m0 : m0 + half, :].rearrange("p m j -> p (m j)"),
-            )
+        def quantise_w1_half(woven, m0):
+            for t in range(PACK):
+                cols = slice(P * t + m0, P * t + m0 + half)
+                quantise(w1_codes[1][:, cols], w1_scales[1][:, cols], woven[:, t].rearrange("p m j -> p (m j)"))
 
-        for t in range(PACK):
-            quantise_w1_half(t, 0)
-        for a, b in ((0, 2), (2, 4)):
-            nc.vector.tensor_copy(grouped1[:, half : half + M_LATE, :, a:b], raw1b[:, 0:M_LATE, :, a:b])
-            nc.scalar.copy(grouped1[:, half + M_LATE : P, :, a:b], raw1b[:, M_LATE:half, :, a:b])
-        for t in range(PACK):
-            quantise_w1_half(t, half)
-        xg1b = keep.tile([P, SLICE, PACK], BF16, align_bytes=64, name="xg1b", tag="late")
-        xg1c = keep.tile([P, 3 * SLICE + SLICE // PACK, PACK], BF16, align_bytes=64, name="xg1c", tag="w1_grouped1")
-        weave_all(nc.scalar.copy, xg1b[:], picked1[:, :, 2 * SLICE : 3 * SLICE])
-        weave_all(nc.vector.tensor_copy, xg1c[:, 0:SLICE, :], picked1[:, :, 3 * SLICE : 4 * SLICE])
+        nc.vector.tensor_copy(woven1a[:, 0:M_EARLY], raw1a[:, 0:M_EARLY])
+        nc.scalar.copy(woven1a[:, M_EARLY:half], raw1a[:, M_EARLY:half])
+        quantise(x_codes1a[:, SLICE:THIRD], x_scales1[:, SLICE:THIRD], flat(x_woven1a[:, SLICE:THIRD, :]))
+        quantise_w1_half(w1_woven1a, 0)
+        for a in (0, 2):
+            nc.vector.tensor_copy(woven1b[:, 0:M_LATE, :, a : a + 2], raw1b[:, 0:M_LATE, :, a : a + 2])
+            nc.scalar.copy(woven1b[:, M_LATE:half, :, a : a + 2], raw1b[:, M_LATE:half, :, a : a + 2])
+        quantise_w1_half(w1_woven1b, half)
 
-        def quantise_x1(i, src):
-            cols = slice(i * SLICE, (i + 1) * SLICE)
-            quantise(x_codes[1][:, cols], x_scales1[:, cols], src.rearrange("p n t -> p (n t)"))
+        x_woven1b = keep.tile([P, S - THIRD, PACK], BF16, align_bytes=64, name="x_woven1b", tag="last_raw")
+        x_codes1b = keep.tile([P, S - THIRD], U32, align_bytes=64, name="x_codes1b")
 
-        quantise_x1(2, xg1b[:])
-        weave_all(nc.vector.tensor_copy, xg1c[:, SLICE : 2 * SLICE, :], picked1[:, :, 4 * SLICE : 5 * SLICE])
-        quantise_x1(3, xg1c[:, 0:SLICE, :])
-        last_row = xg1c[:, 3 * SLICE : 3 * SLICE + SLICE // PACK, :].rearrange("p n t -> p (n t)")
-        nc.vector.tensor_copy(last_row, planes[7].indirect(entries(S - SLICE, S)))
-        quantise_x1(4, xg1c[:, SLICE : 2 * SLICE, :])
-        last = xg1c[:, 2 * SLICE : 3 * SLICE, :]
-        nc.vector.tensor_copy(last[:, :, 0:3], picked1[:, 0:3, S - SLICE : S].rearrange("p t n -> p n t"))
-        nc.vector.tensor_copy(last[:, :, 3], last_row)
-        w2_grouped = keep.tile([P, N, PACK], BF16, align_bytes=64, name="w2_grouped")
+        def weave_late(copy, i):
+            cols = slice((i - 2) * SLICE, (i - 1) * SLICE)
+            weave_all(copy, x_woven1b[:, cols, :], picked1[:, :, i * SLICE : (i + 1) * SLICE])
+
+        def quantise_late(i):
+            cols = slice((i - 2) * SLICE, (i - 1) * SLICE)
+            quantise(x_codes1b[:, cols], x_scales1[:, i * SLICE : (i + 1) * SLICE], flat(x_woven1b[:, cols, :]))
+
+        w2_woven = keep.tile([P, N, PACK], BF16, align_bytes=64, name="w2_woven", tag="last_woven")
         w2_codes = keep.tile([P, N], U32, align_bytes=64, name="w2_codes")
         w2_scales = keep.tile([P, N], U8, align_bytes=64, name="w2_scales")
-        weave_all(nc.vector.tensor_copy, w2_grouped[:], w2_raw[:])
-        quantise_x1(5, last)
-        quantise(w2_codes[:], w2_scales[:], w2_grouped[:].rearrange("p n j -> p (n j)"))
+        weave_late(nc.scalar.copy, 2)
+        weave_late(nc.vector.tensor_copy, 3)
+        quantise_late(2)
+        weave_late(nc.vector.tensor_copy, 4)
+        quantise_late(3)
+        weave_late(nc.vector.tensor_copy, 5)
+        quantise_late(4)
+        weave_all(nc.vector.tensor_copy, w2_woven[:], w2_raw[:])
+        quantise_late(5)
+        quantise(w2_codes[:], w2_scales[:], flat(w2_woven[:]))
 
         h = keep.tile([P, S, PACK], BF16, align_bytes=64, name="h")
         for i in range(SLICES):
-            layer1(i, 1)
+            cols = slice(i * SLICE, (i + 1) * SLICE)
+            codes = x_codes1a[:, cols] if i < 2 else x_codes1b[:, (i - 2) * SLICE : (i - 1) * SLICE]
+            for t in range(PACK):
+                layer1(i, 1, t, codes, x_scales1[:, cols])
             pieces = ((0, SLICE),) if i < SLICES - 1 else ((0, SLICE // 2), (SLICE // 2, SLICE))
             for a, b in pieces:
                 nc.scalar.activation(
-                    h[:, i * SLICE + a : i * SLICE + b, :], acc[i][:, :, a:b].rearrange("p t n -> p n t"), GELU, bias=dummy_out[:] if i == 0 else 0.0
+                    h[:, i * SLICE + a : i * SLICE + b, :], acc[i][:, :, a:b].rearrange("p t n -> p n t"), GELU
                 )
 
         h_codes = keep.tile([P, S], U32, align_bytes=64, name="h_codes")

@@ -24,7 +24,8 @@ PASSES = K // K_PASS
 SLICE = 128
 SLICES = S // SLICE
 THIRD = S // 3
-M_EARLY = 40
+M_PASS0 = 80
+M_EARLY = 44
 M_LATE = 40
 
 
@@ -108,21 +109,18 @@ def tile_picked_sub_mlp_gelu_sub_e_kernel(
 
         picked1 = keep.tile([P, PACK, S], F32, name="picked1")
         nc.vector.tensor_copy(picked1[:, 0, :], picked_from(rows[4], 0, S))
-        for t in (1, 2):
-            scalar_gather(picked1[:, t, :], picked_from(rows[4 + t], 0, S))
+        scalar_gather(picked1[:, 1, :], picked_from(rows[5], 0, S))
+        nc.vector.tensor_copy(picked1[:, 2, 0:THIRD], picked_from(rows[6], 0, THIRD))
+        scalar_gather(picked1[:, 2, THIRD:S], picked_from(rows[6], THIRD, S))
 
         w1_codes = [keep.tile([P, H], U32, align_bytes=64, name=f"w1_codes{s}") for s in range(PASSES)]
         w1_scales = [keep.tile([P, H], U8, align_bytes=64, name=f"w1_scales{s}") for s in range(PASSES)]
-        w1_woven0 = keep.tile([P, PACK, P, PACK], BF16, align_bytes=64, name="w1_woven0", tag="early")
+        w1_woven0 = keep.tile([P, PACK, P, PACK], BF16, align_bytes=64, name="w1_woven0")
         raw0 = w1_raw0[:].rearrange("p j (m t) -> p m j t", t=PACK)
         woven0 = w1_woven0[:].rearrange("p t m j -> p m j t")
-        for a in (0, 2):
-            nc.vector.tensor_copy(woven0[:, :, :, a : a + 2], raw0[:, :, :, a : a + 2])
-        for a in (0, 2):
-            cols = slice(a * P, (a + 2) * P)
-            quantise(
-                w1_codes[0][:, cols], w1_scales[0][:, cols], w1_woven0[:, a : a + 2].rearrange("p t m j -> p (t m j)")
-            )
+        nc.vector.tensor_copy(woven0[:, 0:M_PASS0], raw0[:, 0:M_PASS0])
+        nc.scalar.copy(woven0[:, M_PASS0:P], raw0[:, M_PASS0:P])
+        quantise(w1_codes[0][:], w1_scales[0][:], w1_woven0[:].rearrange("p t m j -> p (t m j)"))
 
         acc = [banks.tile([P, PACK, SLICE], F32, name=f"acc{i}", tag=f"acc{i}") for i in range(SLICES)]
 
@@ -137,15 +135,15 @@ def tile_picked_sub_mlp_gelu_sub_e_kernel(
                 stop=(s == PASSES - 1 and t == PACK - 1),
             )
 
-        for t in range(PACK):
-            for i in range(SLICES):
-                cols = slice(i * SLICE, (i + 1) * SLICE)
+        for i in range(SLICES):
+            cols = slice(i * SLICE, (i + 1) * SLICE)
+            for t in range(PACK):
                 layer1(i, 0, t, x_codes0[:, cols], x_scales0[:, cols])
 
         scalar_gather(picked1[:, 3, THIRD:S], picked_from(rows[7], THIRD, S))
         x_scales1 = keep.tile([P, S], U8, align_bytes=64, name="x_scales1")
         x_codes1a = keep.tile([P, THIRD], U32, align_bytes=64, name="x_codes1a")
-        x_woven1a = keep.tile([P, THIRD, PACK], BF16, align_bytes=64, name="x_woven1a", tag="early")
+        x_woven1a = keep.tile([P, THIRD, PACK], BF16, align_bytes=64, name="x_woven1a")
         nc.vector.tensor_copy(x_woven1a[:, :, 0:3], picked1[:, 0:3, 0:THIRD].rearrange("p t n -> p n t"))
         nc.vector.tensor_copy(x_woven1a[:, :, 3], picked_from(rows[7], 0, THIRD))
         quantise(x_codes1a[:, 0:SLICE], x_scales1[:, 0:SLICE], flat(x_woven1a[:, 0:SLICE, :]))
@@ -233,10 +231,13 @@ def tile_picked_sub_mlp_gelu_sub_e_kernel(
         terms = [keep.tile([P, V], F32, name=f"term{d}") for d in range(D)]
         pair = keep.tile([P, V], F32, name="pair")
         total = keep.tile([P, V], F32, name="total")
-        for cols in blocks:
-            for d in (1, 2):
-                window = y[:].indirect(places[d][:, cols.start // 16 : cols.stop // 16])
-                nc.scalar.activation(fetched[:, d - 1, cols], window, COPY)
+
+        def looked_up(d, b):
+            return y[:].indirect(places[d][:, blocks[b].start // 16 : blocks[b].stop // 16])
+
+        for d, b in ((2, 0), (1, 1), (2, 1), (1, 2), (2, 2)):
+            nc.scalar.activation(fetched[:, d - 1, blocks[b]], looked_up(d, b), COPY)
+        nc.vector.tensor_tensor(terms[1][:, blocks[0]], looked_up(1, 0), gates[:, 1, blocks[0]], MULT)
         nc.vector.tensor_tensor(terms[0][:], y[:].indirect(places[0][:]), gates[:, 0, :], MULT)
 
         def weigh(d, b):
@@ -248,7 +249,6 @@ def tile_picked_sub_mlp_gelu_sub_e_kernel(
         def add_third(b):
             nc.vector.tensor_add(total[:, blocks[b]], pair[:, blocks[b]], terms[2][:, blocks[b]])
 
-        weigh(1, 0)
         weigh(2, 0)
         weigh(1, 1)
         add_pair(0)

@@ -25,8 +25,7 @@ SLICE = 128
 SLICES = S // SLICE
 THIRD = S // 3
 M_PASS0 = 80
-M_EARLY = 44
-M_LATE = 40
+M_LATE = 84
 
 
 def tile_picked_sub_mlp_gelu_sub_e_kernel(
@@ -60,10 +59,10 @@ def tile_picked_sub_mlp_gelu_sub_e_kernel(
         w1_raw0 = keep.tile([P, PACK, H], F32, align_bytes=64, name="w1_raw0")
         nc.sync.dma_start(w1_raw0[:], w1_rows(0))
         rows.extend(load_rows(1, 3, 1))
-        w1_raw1a = keep.tile([P, PACK, H // 2], F32, align_bytes=64, name="w1_raw1a")
-        nc.sync.dma_start(w1_raw1a[:], w1_rows(1)[:, :, 0 : H // 2])
-        w1_raw1b = keep.tile([P, PACK, H // 2], F32, align_bytes=64, name="w1_raw1b", tag="last_raw")
-        nc.sync.dma_start(w1_raw1b[:], w1_rows(1)[:, :, H // 2 : H])
+        w1_raw1a = keep.tile([P, 2, H], F32, align_bytes=64, name="w1_raw1a")
+        nc.sync.dma_start(w1_raw1a[:], w1_rows(1)[:, 0:2, :])
+        w1_raw1b = keep.tile([P, 2, H], F32, align_bytes=64, name="w1_raw1b", tag="last_raw")
+        nc.sync.dma_start(w1_raw1b[:], w1_rows(1)[:, 2:4, :])
         w2_raw = keep.tile([P, PACK, N], F32, name="w2_raw")
         nc.sync.dma_start(w2_raw[:], w2.rearrange("(p j) n -> p j n", j=PACK))
         places = []
@@ -148,27 +147,19 @@ def tile_picked_sub_mlp_gelu_sub_e_kernel(
         nc.vector.tensor_copy(x_woven1a[:, :, 3], picked_from(rows[7], 0, THIRD))
         quantise(x_codes1a[:, 0:SLICE], x_scales1[:, 0:SLICE], flat(x_woven1a[:, 0:SLICE, :]))
 
-        half = P // 2
-        w1_woven1a = keep.tile([P, PACK, half, PACK], BF16, align_bytes=64, name="w1_woven1a")
-        w1_woven1b = keep.tile([P, PACK, half, PACK], BF16, align_bytes=64, name="w1_woven1b", tag="last_woven")
-        raw1a = w1_raw1a[:].rearrange("p j (m t) -> p m j t", t=PACK)
-        raw1b = w1_raw1b[:].rearrange("p j (m t) -> p m j t", t=PACK)
-        woven1a = w1_woven1a[:].rearrange("p t m j -> p m j t")
-        woven1b = w1_woven1b[:].rearrange("p t m j -> p m j t")
-
-        def quantise_w1_half(woven, m0):
-            for t in range(PACK):
-                cols = slice(P * t + m0, P * t + m0 + half)
-                quantise(w1_codes[1][:, cols], w1_scales[1][:, cols], woven[:, t].rearrange("p m j -> p (m j)"))
-
-        nc.vector.tensor_copy(woven1a[:, 0:M_EARLY], raw1a[:, 0:M_EARLY])
-        nc.scalar.copy(woven1a[:, M_EARLY:half], raw1a[:, M_EARLY:half])
+        w1_woven1 = keep.tile([P, PACK, P, PACK], BF16, align_bytes=64, name="w1_woven1", tag="last_woven")
+        raw1a = w1_raw1a[:].rearrange("p j (m t) -> p m t j", t=PACK)
+        raw1b = w1_raw1b[:].rearrange("p j (m t) -> p m t j", t=PACK)
+        woven1 = w1_woven1[:].rearrange("p t m j -> p m t j")
+        nc.vector.tensor_copy(woven1[:, 0:M_LATE, :, 0:2], raw1a[:, 0:M_LATE])
+        nc.scalar.copy(woven1[:, M_LATE:P, :, 0:2], raw1a[:, M_LATE:P])
         quantise(x_codes1a[:, SLICE:THIRD], x_scales1[:, SLICE:THIRD], flat(x_woven1a[:, SLICE:THIRD, :]))
-        quantise_w1_half(w1_woven1a, 0)
         for a in (0, 2):
-            nc.vector.tensor_copy(woven1b[:, 0:M_LATE, :, a : a + 2], raw1b[:, 0:M_LATE, :, a : a + 2])
-            nc.scalar.copy(woven1b[:, M_LATE:half, :, a : a + 2], raw1b[:, M_LATE:half, :, a : a + 2])
-        quantise_w1_half(w1_woven1b, half)
+            nc.vector.tensor_copy(woven1[:, 0:M_LATE, a : a + 2, 2:4], raw1b[:, 0:M_LATE, a : a + 2])
+            nc.scalar.copy(woven1[:, M_LATE:P, a : a + 2, 2:4], raw1b[:, M_LATE:P, a : a + 2])
+        for t in range(PACK):
+            cols = slice(P * t, P * (t + 1))
+            quantise(w1_codes[1][:, cols], w1_scales[1][:, cols], w1_woven1[:, t].rearrange("p m j -> p (m j)"))
 
         x_woven1b = keep.tile([P, S - THIRD, PACK], BF16, align_bytes=64, name="x_woven1b", tag="last_raw")
         x_codes1b = keep.tile([P, S - THIRD], U32, align_bytes=64, name="x_codes1b")

@@ -25,6 +25,7 @@ SLICE = 128
 SLICES = S // SLICE
 THIRD = S // 3
 M_PASS0 = 80
+M_EARLY = 96
 M_LATE = 84
 
 
@@ -141,41 +142,45 @@ def tile_picked_sub_mlp_gelu_sub_e_kernel(
 
         scalar_gather(picked1[:, 3, THIRD:S], picked_from(rows[7], THIRD, S))
         x_scales1 = keep.tile([P, S], U8, align_bytes=64, name="x_scales1")
-        x_codes1a = keep.tile([P, THIRD], U32, align_bytes=64, name="x_codes1a")
-        x_woven1a = keep.tile([P, THIRD, PACK], BF16, align_bytes=64, name="x_woven1a")
+        x_codes1a = keep.tile([P, SLICE], U32, align_bytes=64, name="x_codes1a")
+        x_woven1a = keep.tile([P, THIRD, PACK], BF16, align_bytes=64, name="x_woven1a", tag="slices01")
         nc.vector.tensor_copy(x_woven1a[:, :, 0:3], picked1[:, 0:3, 0:THIRD].rearrange("p t n -> p n t"))
         nc.vector.tensor_copy(x_woven1a[:, :, 3], picked_from(rows[7], 0, THIRD))
-        quantise(x_codes1a[:, 0:SLICE], x_scales1[:, 0:SLICE], flat(x_woven1a[:, 0:SLICE, :]))
+        quantise(x_codes1a[:], x_scales1[:, 0:SLICE], flat(x_woven1a[:, 0:SLICE, :]))
 
-        w1_woven1 = keep.tile([P, PACK, P, PACK], BF16, align_bytes=64, name="w1_woven1", tag="last_woven")
-        raw1a = w1_raw1a[:].rearrange("p j (m t) -> p m t j", t=PACK)
-        raw1b = w1_raw1b[:].rearrange("p j (m t) -> p m t j", t=PACK)
-        woven1 = w1_woven1[:].rearrange("p t m j -> p m t j")
-        nc.vector.tensor_copy(woven1[:, 0:M_LATE, :, 0:2], raw1a[:, 0:M_LATE])
-        nc.scalar.copy(woven1[:, M_LATE:P, :, 0:2], raw1a[:, M_LATE:P])
-        quantise(x_codes1a[:, SLICE:THIRD], x_scales1[:, SLICE:THIRD], flat(x_woven1a[:, SLICE:THIRD, :]))
-        for a in (0, 2):
-            nc.vector.tensor_copy(woven1[:, 0:M_LATE, a : a + 2, 2:4], raw1b[:, 0:M_LATE, a : a + 2])
-            nc.scalar.copy(woven1[:, M_LATE:P, a : a + 2, 2:4], raw1b[:, M_LATE:P, a : a + 2])
-        for t in range(PACK):
-            cols = slice(P * t, P * (t + 1))
-            quantise(w1_codes[1][:, cols], w1_scales[1][:, cols], w1_woven1[:, t].rearrange("p m j -> p (m j)"))
+        raw1 = [raw[:].rearrange("p j (m t) -> p m t j", t=PACK) for raw in (w1_raw1a, w1_raw1b)]
+        w1_woven1 = [
+            keep.tile([P, 2, P, PACK], BF16, align_bytes=64, name="w1_woven1_01", tag="last_woven"),
+            keep.tile([P, 2, P, PACK], BF16, align_bytes=64, name="w1_woven1_23"),
+        ]
+        for load, share in enumerate((M_EARLY, M_LATE)):
+            for pair in range(2):
+                dst = w1_woven1[pair][:].rearrange("p t m j -> p m t j")[:, :, :, 2 * load : 2 * load + 2]
+                src = raw1[load][:, :, 2 * pair : 2 * pair + 2]
+                nc.vector.tensor_copy(dst[:, 0:share], src[:, 0:share])
+                nc.scalar.copy(dst[:, share:P], src[:, share:P])
+        for a, b in ((0, 2), (2, 3), (3, 4)):
+            cols = slice(P * a, P * b)
+            woven = w1_woven1[a // 2][:, a % 2 : a % 2 + b - a].rearrange("p t m j -> p (t m j)")
+            quantise(w1_codes[1][:, cols], w1_scales[1][:, cols], woven)
 
         x_woven1b = keep.tile([P, S - THIRD, PACK], BF16, align_bytes=64, name="x_woven1b", tag="last_raw")
-        x_codes1b = keep.tile([P, S - THIRD], U32, align_bytes=64, name="x_codes1b")
+        x_codes1b = keep.tile([P, S - SLICE], U32, align_bytes=64, name="x_codes1b", tag="last_woven")
 
         def weave_late(copy, i):
             cols = slice((i - 2) * SLICE, (i - 1) * SLICE)
             weave_all(copy, x_woven1b[:, cols, :], picked1[:, :, i * SLICE : (i + 1) * SLICE])
 
         def quantise_late(i):
-            cols = slice((i - 2) * SLICE, (i - 1) * SLICE)
-            quantise(x_codes1b[:, cols], x_scales1[:, i * SLICE : (i + 1) * SLICE], flat(x_woven1b[:, cols, :]))
+            woven = x_woven1a[:, SLICE:THIRD, :] if i == 1 else x_woven1b[:, (i - 2) * SLICE : (i - 1) * SLICE, :]
+            codes = x_codes1b[:, (i - 1) * SLICE : i * SLICE]
+            quantise(codes, x_scales1[:, i * SLICE : (i + 1) * SLICE], flat(woven))
 
-        w2_woven = keep.tile([P, N, PACK], BF16, align_bytes=64, name="w2_woven", tag="last_woven")
+        w2_woven = keep.tile([P, N, PACK], BF16, align_bytes=64, name="w2_woven", tag="slices01")
         w2_codes = keep.tile([P, N], U32, align_bytes=64, name="w2_codes")
         w2_scales = keep.tile([P, N], U8, align_bytes=64, name="w2_scales")
         weave_late(nc.scalar.copy, 2)
+        quantise_late(1)
         weave_late(nc.vector.tensor_copy, 3)
         quantise_late(2)
         weave_late(nc.vector.tensor_copy, 4)
@@ -189,7 +194,7 @@ def tile_picked_sub_mlp_gelu_sub_e_kernel(
         h = keep.tile([P, S, PACK], BF16, align_bytes=64, name="h")
         for i in range(SLICES):
             cols = slice(i * SLICE, (i + 1) * SLICE)
-            codes = x_codes1a[:, cols] if i < 2 else x_codes1b[:, (i - 2) * SLICE : (i - 1) * SLICE]
+            codes = x_codes1a[:] if i == 0 else x_codes1b[:, (i - 1) * SLICE : i * SLICE]
             for t in range(PACK):
                 layer1(i, 1, t, codes, x_scales1[:, cols])
             pieces = ((0, SLICE),) if i < SLICES - 1 else ((0, SLICE // 2), (SLICE // 2, SLICE))

@@ -24,8 +24,8 @@ PASSES = K // K_PASS
 SLICE = 128
 SLICES = S // SLICE
 THIRD = S // 3
-M_PASS0 = 80
-M_EARLY = 96
+M_PASS0 = 84
+M_EARLY = 84
 M_LATE = 84
 
 
@@ -107,108 +107,137 @@ def tile_picked_sub_mlp_gelu_sub_e_kernel(
         for a, b in ((0, cut), (cut, S)):
             quantise(x_codes0[:, a:b], x_scales0[:, a:b], flat(x_woven0[:, a:b, :]))
 
+        thirds = [slice(i * THIRD, (i + 1) * THIRD) for i in range(3)]
         picked1 = keep.tile([P, PACK, S], F32, name="picked1")
+        x_woven1 = [keep.tile([P, THIRD, PACK], BF16, align_bytes=64, name=f"x_woven1{i}") for i in range(2)]
+        x_codes1 = []
+        x_scales1 = keep.tile([P, S], U8, align_bytes=64, name="x_scales1")
+
+        def weave_pair(copy, i, t):
+            copy(x_woven1[i][:, :, t : t + 2], picked1[:, t : t + 2, thirds[i]].rearrange("p t n -> p n t"))
+
         nc.vector.tensor_copy(picked1[:, 0, :], picked_from(rows[4], 0, S))
         scalar_gather(picked1[:, 1, :], picked_from(rows[5], 0, S))
-        nc.vector.tensor_copy(picked1[:, 2, 0:THIRD], picked_from(rows[6], 0, THIRD))
+        for i in range(2):
+            weave_pair(nc.vector.tensor_copy, i, 0)
+        nc.vector.tensor_copy(x_woven1[0][:, :, 2], picked_from(rows[6], 0, THIRD))
         scalar_gather(picked1[:, 2, THIRD:S], picked_from(rows[6], THIRD, S))
 
         w1_codes = [keep.tile([P, H], U32, align_bytes=64, name=f"w1_codes{s}") for s in range(PASSES)]
         w1_scales = [keep.tile([P, H], U8, align_bytes=64, name=f"w1_scales{s}") for s in range(PASSES)]
-        w1_woven0 = keep.tile([P, PACK, P, PACK], BF16, align_bytes=64, name="w1_woven0")
-        raw0 = w1_raw0[:].rearrange("p j (m t) -> p m j t", t=PACK)
-        woven0 = w1_woven0[:].rearrange("p t m j -> p m j t")
-        nc.vector.tensor_copy(woven0[:, 0:M_PASS0], raw0[:, 0:M_PASS0])
-        nc.scalar.copy(woven0[:, M_PASS0:P], raw0[:, M_PASS0:P])
-        quantise(w1_codes[0][:], w1_scales[0][:], w1_woven0[:].rearrange("p t m j -> p (t m j)"))
-
-        acc = [banks.tile([P, PACK, SLICE], F32, name=f"acc{i}", tag=f"acc{i}") for i in range(SLICES)]
-
-        def layer1(i, s, t, codes, scales):
-            nc.tensor.matmul_mx(
-                out=acc[i][:, t, :],
-                lhsT=w1_codes[s][:, t * P : (t + 1) * P].bitcast(FP8X4),
-                lhsT_scale=w1_scales[s][:, t * P : (t + 1) * P],
-                rhs=codes.bitcast(FP8X4),
-                rhs_scale=scales,
-                start=(s == 0 and t == 0),
-                stop=(s == PASSES - 1 and t == PACK - 1),
-            )
-
-        for i in range(SLICES):
-            cols = slice(i * SLICE, (i + 1) * SLICE)
-            for t in range(PACK):
-                layer1(i, 0, t, x_codes0[:, cols], x_scales0[:, cols])
-
-        scalar_gather(picked1[:, 3, THIRD:S], picked_from(rows[7], THIRD, S))
-        x_scales1 = keep.tile([P, S], U8, align_bytes=64, name="x_scales1")
-        x_codes1a = keep.tile([P, SLICE], U32, align_bytes=64, name="x_codes1a")
-        x_woven1a = keep.tile([P, THIRD, PACK], BF16, align_bytes=64, name="x_woven1a", tag="slices01")
-        nc.vector.tensor_copy(x_woven1a[:, :, 0:3], picked1[:, 0:3, 0:THIRD].rearrange("p t n -> p n t"))
-        nc.vector.tensor_copy(x_woven1a[:, :, 3], picked_from(rows[7], 0, THIRD))
-        quantise(x_codes1a[:], x_scales1[:, 0:SLICE], flat(x_woven1a[:, 0:SLICE, :]))
-
-        raw1 = [raw[:].rearrange("p j (m t) -> p m t j", t=PACK) for raw in (w1_raw1a, w1_raw1b)]
-        w1_woven1 = [
-            keep.tile([P, 2, P, PACK], BF16, align_bytes=64, name="w1_woven1_01", tag="last_woven"),
-            keep.tile([P, 2, P, PACK], BF16, align_bytes=64, name="w1_woven1_23"),
+        w1_woven = [
+            [
+                keep.tile([P, 2, P, PACK], BF16, align_bytes=64, name=f"w1_woven{s}{pair}", tag=f"w1_woven{s}{pair}")
+                for pair in range(2)
+            ]
+            for s in range(PASSES)
         ]
-        for load, share in enumerate((M_EARLY, M_LATE)):
-            for pair in range(2):
-                dst = w1_woven1[pair][:].rearrange("p t m j -> p m t j")[:, :, :, 2 * load : 2 * load + 2]
-                src = raw1[load][:, :, 2 * pair : 2 * pair + 2]
-                nc.vector.tensor_copy(dst[:, 0:share], src[:, 0:share])
-                nc.scalar.copy(dst[:, share:P], src[:, share:P])
-        for a, b in ((0, 2), (2, 3), (3, 4)):
-            cols = slice(P * a, P * b)
-            woven = w1_woven1[a // 2][:, a % 2 : a % 2 + b - a].rearrange("p t m j -> p (t m j)")
-            quantise(w1_codes[1][:, cols], w1_scales[1][:, cols], woven)
 
-        x_woven1b = keep.tile([P, S - THIRD, PACK], BF16, align_bytes=64, name="x_woven1b", tag="last_raw")
-        x_codes1b = keep.tile([P, S - SLICE], U32, align_bytes=64, name="x_codes1b", tag="last_woven")
+        def weave_part(copy, s, pair, raw, j0, j1, m0, m1):
+            dst = w1_woven[s][pair][:].rearrange("p t m j -> p m t j")[:, :, :, j0:j1]
+            src = raw[:].rearrange("p j (m t) -> p m t j", t=PACK)[:, :, 2 * pair : 2 * pair + 2]
+            copy(dst[:, m0:m1], src[:, m0:m1])
 
-        def weave_late(copy, i):
-            cols = slice((i - 2) * SLICE, (i - 1) * SLICE)
-            weave_all(copy, x_woven1b[:, cols, :], picked1[:, :, i * SLICE : (i + 1) * SLICE])
+        def weave_w1(s, pair, raw, j0, j1, share):
+            weave_part(nc.vector.tensor_copy, s, pair, raw, j0, j1, 0, share)
+            weave_part(nc.scalar.copy, s, pair, raw, j0, j1, share, P)
 
-        def quantise_late(i):
-            woven = x_woven1a[:, SLICE:THIRD, :] if i == 1 else x_woven1b[:, (i - 2) * SLICE : (i - 1) * SLICE, :]
-            codes = x_codes1b[:, (i - 1) * SLICE : i * SLICE]
-            quantise(codes, x_scales1[:, i * SLICE : (i + 1) * SLICE], flat(woven))
+        def quantise_w1(s, a, b):
+            woven = w1_woven[s][a // 2][:, a % 2 : a % 2 + b - a].rearrange("p t m j -> p (t m j)")
+            quantise(w1_codes[s][:, P * a : P * b], w1_scales[s][:, P * a : P * b], woven)
 
-        w2_woven = keep.tile([P, N, PACK], BF16, align_bytes=64, name="w2_woven", tag="slices01")
+        def quantise_third(i, woven, tag):
+            codes = keep.tile([P, THIRD], U32, align_bytes=64, name=f"x_codes1{i}", tag=tag)
+            quantise(codes[:], x_scales1[:, thirds[i]], flat(woven[:]))
+            x_codes1.append(codes)
+
+        for pair in range(2):
+            weave_w1(0, pair, w1_raw0, 0, PACK, M_PASS0)
+        for pair in range(2):
+            quantise_w1(0, 2 * pair, 2 * pair + 2)
+
+        nc.vector.tensor_copy(x_woven1[0][:, :, 3], picked_from(rows[7], 0, THIRD))
+        for i in (1, 2):
+            scalar_gather(picked1[:, 3, thirds[i]], picked_from(rows[7], thirds[i].start, thirds[i].stop))
+        weave_pair(nc.vector.tensor_copy, 1, 2)
+        quantise_third(0, x_woven1[0], "x_codes10")
+
+        for pair in range(2):
+            weave_w1(1, pair, w1_raw1a, 0, 2, M_EARLY)
+        for pair in range(2):
+            weave_w1(1, pair, w1_raw1b, 2, PACK, M_LATE)
+        for t in range(PACK):
+            quantise_w1(1, t, t + 1)
+        quantise_third(1, x_woven1[1], "w1_woven10")
+        x_woven_last = keep.tile([P, THIRD, PACK], BF16, align_bytes=64, name="x_woven_last", tag="last_raw")
+        for i, copy in ((0, nc.scalar.copy), (1, nc.vector.tensor_copy)):
+            cols = slice(2 * THIRD + i * SLICE, 2 * THIRD + (i + 1) * SLICE)
+            weave_all(copy, x_woven_last[:, i * SLICE : (i + 1) * SLICE, :], picked1[:, :, cols])
+        quantise_third(2, x_woven_last, "x_codes12")
+
+        w2_woven = keep.tile([P, N, PACK], BF16, align_bytes=64, name="w2_woven")
         w2_codes = keep.tile([P, N], U32, align_bytes=64, name="w2_codes")
         w2_scales = keep.tile([P, N], U8, align_bytes=64, name="w2_scales")
-        weave_late(nc.scalar.copy, 2)
-        quantise_late(1)
-        weave_late(nc.vector.tensor_copy, 3)
-        quantise_late(2)
-        weave_late(nc.vector.tensor_copy, 4)
-        quantise_late(3)
-        weave_late(nc.vector.tensor_copy, 5)
-        quantise_late(4)
         weave_all(nc.vector.tensor_copy, w2_woven[:], w2_raw[:])
-        quantise_late(5)
         quantise(w2_codes[:], w2_scales[:], flat(w2_woven[:]))
 
-        h = keep.tile([P, S, PACK], BF16, align_bytes=64, name="h")
-        for i in range(SLICES):
+
+        def x_codes(s, cols):
+            if s == 0:
+                return x_codes0[:, cols]
+            first = cols.start // THIRD * THIRD
+            return x_codes1[cols.start // THIRD][:, cols.start - first : cols.stop - first]
+
+        x_scales = (x_scales0, x_scales1)
+
+        def layer1(dst, s, t, cols, start, stop):
+            nc.tensor.matmul_mx(
+                out=dst,
+                lhsT=w1_codes[s][:, t * P : (t + 1) * P].bitcast(FP8X4),
+                lhsT_scale=w1_scales[s][:, t * P : (t + 1) * P],
+                rhs=x_codes(s, cols).bitcast(FP8X4),
+                rhs_scale=x_scales[s][:, cols],
+                start=start,
+                stop=stop,
+            )
+
+        batches = ((0, 256, "acc0"), (256, 512, "acc1"), (512, 640, "acc2"), (640, 704, "acc3"), (704, 768, "acc4"))
+        h = {
+            a: keep.tile([P, b - a, PACK], BF16, align_bytes=64, name=f"h{a}", tag=f"h{a}") for a, b, tag in batches
+        }
+
+        def h_part(a, b):
+            first = max(start for start in h if start <= a)
+            return h[first][:, a - first : b - first, :]
+
+        h_rows = keep.tile([P, PACK, THIRD], BF16, align_bytes=64, name="h_rows")
+        groups = ((0, 1), (1, 2), (2, 3), (3, 4))
+        early = [banks.tile([P, b - a, THIRD], F32, name=f"early{a}", tag=f"acc{g}") for g, (a, b) in enumerate(groups)]
+        for s in range(PASSES):
+            for g, (a, b) in enumerate(groups):
+                for t in range(a, b):
+                    layer1(early[g][:, t - a, :], s, t, thirds[0], s == 0 and t == a, s == 1 and t == b - 1)
+        for g, (a, b) in enumerate(groups):
+            nc.scalar.activation(h_rows[:, a:b, :], early[g][:], GELU)
+        weave_all(nc.vector.tensor_copy, h_part(0, THIRD), h_rows[:])
+
+        for i, tag in ((2, "acc4"), (3, "acc5"), (4, "acc6"), (5, "acc7")):
             cols = slice(i * SLICE, (i + 1) * SLICE)
-            codes = x_codes1a[:] if i == 0 else x_codes1b[:, (i - 1) * SLICE : i * SLICE]
-            for t in range(PACK):
-                layer1(i, 1, t, codes, x_scales1[:, cols])
+            acc = banks.tile([P, PACK, SLICE], F32, name=f"acc_slice{i}", tag=tag)
+            for s in range(PASSES):
+                for t in range(PACK):
+                    layer1(acc[:, t, :], s, t, cols, s == 0 and t == 0, s == 1 and t == PACK - 1)
             pieces = ((0, SLICE),) if i < SLICES - 1 else ((0, SLICE // 2), (SLICE // 2, SLICE))
             for a, b in pieces:
                 nc.scalar.activation(
-                    h[:, i * SLICE + a : i * SLICE + b, :], acc[i][:, :, a:b].rearrange("p t n -> p n t"), GELU
+                    h_part(i * SLICE + a, i * SLICE + b), acc[:, :, a:b].rearrange("p t n -> p n t"), GELU
                 )
 
         h_codes = keep.tile([P, S], U32, align_bytes=64, name="h_codes")
         h_scales = keep.tile([P, S], U8, align_bytes=64, name="h_scales")
-        y = keep.tile([P, S], F32, name="y")
-        batches = ((0, 256, "y0"), (256, 512, "y1"), (512, 640, "acc0"), (640, 704, "acc1"), (704, 768, "acc2"))
+        y_parts = []
         for a, b, tag in batches:
-            quantise(h_codes[:, a:b], h_scales[:, a:b], h[:, a:b, :].rearrange("p n t -> p (n t)"))
+            quantise(h_codes[:, a:b], h_scales[:, a:b], flat(h_part(a, b)))
             y_part = banks.tile([P, b - a], F32, name=f"y_part{a}", tag=tag)
             nc.tensor.matmul_mx(
                 out=y_part[:],
@@ -219,8 +248,11 @@ def tile_picked_sub_mlp_gelu_sub_e_kernel(
                 start=True,
                 stop=True,
             )
-            copy = nc.vector.tensor_copy if a == 0 else nc.scalar.copy
-            copy(y[:, a:b], y_part[:])
+            y_parts.append(y_part)
+        y = keep.tile([P, S], F32, align_bytes=64, name="y", tag="h704")
+        for i, (a, b, tag) in enumerate(batches):
+            copy = nc.scalar.copy if i % 2 == 0 else nc.vector.tensor_copy
+            copy(y[:, a:b], y_parts[i][:])
 
         blocks = [slice(i * P, (i + 1) * P) for i in range(V // P)]
         fetched = keep.tile([P, D - 1, V], F32, name="fetched")

@@ -25,7 +25,6 @@ SLICE = 128
 SLICES = S // SLICE
 THIRD = S // 3
 M_PASS0 = 84
-M_EARLY = 84
 M_LATE = 84
 
 
@@ -60,10 +59,8 @@ def tile_picked_sub_mlp_gelu_sub_e_kernel(
         w1_raw0 = keep.tile([P, PACK, H], F32, align_bytes=64, name="w1_raw0")
         nc.sync.dma_start(w1_raw0[:], w1_rows(0))
         rows.extend(load_rows(1, 3, 1))
-        w1_raw1a = keep.tile([P, 2, H], F32, align_bytes=64, name="w1_raw1a")
-        nc.sync.dma_start(w1_raw1a[:], w1_rows(1)[:, 0:2, :])
-        w1_raw1b = keep.tile([P, 2, H], F32, align_bytes=64, name="w1_raw1b", tag="last_raw")
-        nc.sync.dma_start(w1_raw1b[:], w1_rows(1)[:, 2:4, :])
+        w1_raw1 = keep.tile([P, PACK, H], F32, align_bytes=64, name="w1_raw1", tag="last_raw")
+        nc.sync.dma_start(w1_raw1[:], w1_rows(1))
         w2_raw = keep.tile([P, PACK, N], F32, name="w2_raw")
         nc.sync.dma_start(w2_raw[:], w2.rearrange("(p j) n -> p j n", j=PACK))
         places = []
@@ -118,8 +115,7 @@ def tile_picked_sub_mlp_gelu_sub_e_kernel(
 
         nc.vector.tensor_copy(picked1[:, 0, :], picked_from(rows[4], 0, S))
         scalar_gather(picked1[:, 1, :], picked_from(rows[5], 0, S))
-        for i in range(2):
-            weave_pair(nc.vector.tensor_copy, i, 0)
+        weave_pair(nc.vector.tensor_copy, 0, 0)
         nc.vector.tensor_copy(x_woven1[0][:, :, 2], picked_from(rows[6], 0, THIRD))
         scalar_gather(picked1[:, 2, THIRD:S], picked_from(rows[6], THIRD, S))
 
@@ -133,14 +129,11 @@ def tile_picked_sub_mlp_gelu_sub_e_kernel(
             for s in range(PASSES)
         ]
 
-        def weave_part(copy, s, pair, raw, j0, j1, m0, m1):
-            dst = w1_woven[s][pair][:].rearrange("p t m j -> p m t j")[:, :, :, j0:j1]
-            src = raw[:].rearrange("p j (m t) -> p m t j", t=PACK)[:, :, 2 * pair : 2 * pair + 2]
-            copy(dst[:, m0:m1], src[:, m0:m1])
-
-        def weave_w1(s, pair, raw, j0, j1, share):
-            weave_part(nc.vector.tensor_copy, s, pair, raw, j0, j1, 0, share)
-            weave_part(nc.scalar.copy, s, pair, raw, j0, j1, share, P)
+        def weave_w1(s, pair, raw, share):
+            dst = w1_woven[s][pair][:].rearrange("p t m j -> p m j t")
+            src = raw[:].rearrange("p j (m t) -> p m j t", t=PACK)[:, :, :, 2 * pair : 2 * pair + 2]
+            nc.vector.tensor_copy(dst[:, 0:share], src[:, 0:share])
+            nc.scalar.copy(dst[:, share:P], src[:, share:P])
 
         def quantise_w1(s, a, b):
             woven = w1_woven[s][a // 2][:, a % 2 : a % 2 + b - a].rearrange("p t m j -> p (t m j)")
@@ -152,28 +145,29 @@ def tile_picked_sub_mlp_gelu_sub_e_kernel(
             x_codes1.append(codes)
 
         for pair in range(2):
-            weave_w1(0, pair, w1_raw0, 0, PACK, M_PASS0)
+            weave_w1(0, pair, w1_raw0, M_PASS0)
         for pair in range(2):
             quantise_w1(0, 2 * pair, 2 * pair + 2)
 
         nc.vector.tensor_copy(x_woven1[0][:, :, 3], picked_from(rows[7], 0, THIRD))
         for i in (1, 2):
             scalar_gather(picked1[:, 3, thirds[i]], picked_from(rows[7], thirds[i].start, thirds[i].stop))
-        weave_pair(nc.vector.tensor_copy, 1, 2)
         quantise_third(0, x_woven1[0], "x_codes10")
+        weave_all(nc.vector.tensor_copy, x_woven1[1][:], picked1[:, :, thirds[1]])
+        x_woven_last = [keep.tile([P, SLICE, PACK], BF16, align_bytes=64, name="x_woven4")]
+        weave_all(nc.scalar.copy, x_woven_last[0][:], picked1[:, :, 4 * SLICE : 5 * SLICE])
 
         for pair in range(2):
-            weave_w1(1, pair, w1_raw1a, 0, 2, M_EARLY)
-        for pair in range(2):
-            weave_w1(1, pair, w1_raw1b, 2, PACK, M_LATE)
+            weave_w1(1, pair, w1_raw1, M_LATE)
         for t in range(PACK):
             quantise_w1(1, t, t + 1)
         quantise_third(1, x_woven1[1], "w1_woven10")
-        x_woven_last = keep.tile([P, THIRD, PACK], BF16, align_bytes=64, name="x_woven_last", tag="last_raw")
-        for i, copy in ((0, nc.scalar.copy), (1, nc.vector.tensor_copy)):
-            cols = slice(2 * THIRD + i * SLICE, 2 * THIRD + (i + 1) * SLICE)
-            weave_all(copy, x_woven_last[:, i * SLICE : (i + 1) * SLICE, :], picked1[:, :, cols])
-        quantise_third(2, x_woven_last, "x_codes12")
+        x_woven_last.append(keep.tile([P, SLICE, PACK], BF16, align_bytes=64, name="x_woven5", tag="last_raw"))
+        weave_all(nc.vector.tensor_copy, x_woven_last[1][:], picked1[:, :, 5 * SLICE : S])
+        x_codes1.append(keep.tile([P, THIRD], U32, align_bytes=64, name="x_codes12", tag="w1_woven11"))
+        for i in range(2):
+            cols = slice((4 + i) * SLICE, (5 + i) * SLICE)
+            quantise(x_codes1[2][:, i * SLICE : (i + 1) * SLICE], x_scales1[:, cols], flat(x_woven_last[i][:]))
 
         w2_woven = keep.tile([P, N, PACK], BF16, align_bytes=64, name="w2_woven")
         w2_codes = keep.tile([P, N], U32, align_bytes=64, name="w2_codes")

from contextlib import ExitStack

import concourse.mybir as mybir

K, T, D, S, V, H, N = 1024, 2048, 3, 768, 384, 512, 128
FLOPS = 2 * K * H * S + 2 * H * N * S

F32 = mybir.dt.float32
BF16 = mybir.dt.bfloat16
U32 = mybir.dt.uint32
U16 = mybir.dt.uint16
U8 = mybir.dt.uint8
FP8X4 = mybir.dt.float8_e4m3fn_x4
MULT = mybir.AluOpType.mult
ADD = mybir.AluOpType.add
GELU = mybir.ActivationFunctionType.Gelu_apprx_tanh
COPY = mybir.ActivationFunctionType.Copy
IDENTITY = mybir.ActivationFunctionType.Identity

P = 128
PACK = 4
K_PASS = P * PACK
PASSES = K // K_PASS
SLICE = 128
SLICES = S // SLICE
THIRD = S // 3
M_PASS0 = 84
M_LATE = 84


def tile_picked_sub_mlp_gelu_sub_e_kernel(
    tc, xT, w1, w2, gate, offs, pos1, pos2, pos3, out
):
    nc = tc.nc
    with ExitStack() as ctx:
        keep = ctx.enter_context(tc.tile_pool(name="keep", bufs=1))
        banks = ctx.enter_context(tc.psum_pool(name="banks", bufs=1))

        zero = keep.tile([P, 1], F32, name="zero")
        nc.vector.memset(zero[:], 0.0)
        gelu_zero = keep.tile([P, 1], F32, name="gelu_zero")
        nc.scalar.activation(gelu_zero[:], zero[:], GELU)

        def load_rows(s, t, count):
            rows = xT[s * K_PASS : (s + 1) * K_PASS, :].rearrange("(p t) c -> p t c", t=PACK)
            group = keep.tile([P, count, T], F32, align_bytes=64, name=f"rows{s}{t}")
            nc.sync.dma_start(group[:], rows[:, t : t + count, :])
            return [group[:, i, :] for i in range(count)]

        def w1_rows(s):
            return w1[s * K_PASS : (s + 1) * K_PASS, :].rearrange("(p j) c -> p j c", j=PACK)

        rows = load_rows(0, 0, 2)
        offsets = keep.tile([P, S // 16], U16, name="offsets")
        nc.sync.dma_start(offsets[:], offs)
        rows.extend(load_rows(0, 2, 2))
        rows.extend(load_rows(1, 0, 2))
        rows.extend(load_rows(1, 2, 1))
        w1_raw0 = keep.tile([P, PACK, H], F32, align_bytes=64, name="w1_raw0")
        nc.sync.dma_start(w1_raw0[:], w1_rows(0))
        rows.extend(load_rows(1, 3, 1))
        w1_raw1 = keep.tile([P, PACK, H], F32, align_bytes=64, name="w1_raw1", tag="last_raw")
        nc.sync.dma_start(w1_raw1[:], w1_rows(1))
        w2_raw = keep.tile([P, PACK, N], F32, name="w2_raw")
        nc.sync.dma_start(w2_raw[:], w2.rearrange("(p j) n -> p j n", j=PACK))
        places = []
        for d, pos in enumerate((pos1, pos2, pos3)):
            place = keep.tile([P, V // 16], U16, name=f"place{d}")
            nc.sync.dma_start(place[:], pos)
            places.append(place)
        gates = keep.tile([P, D, V], F32, name="gates")
        nc.sync.dma_start(gates[:], gate.rearrange("d m v -> m d v"))

        def quantise(codes, scales, woven):
            nc.vector.quantize_mx(out=codes.bitcast(FP8X4), scales=scales, in_=woven)

        def picked_from(row, a, b):
            return row.indirect(offsets[:, a // 16 : b // 16])

        def scalar_gather(dst, src):
            nc.scalar.activation(dst, src, COPY)

        def weave_all(copy, dst, src):
            copy(
                dst.rearrange("p (c i) t -> p c t i", i=4),
                src.rearrange("p t (c i) -> p c t i", i=4),
            )

        def flat(woven):
            return woven.rearrange("p n t -> p (n t)")

        x_codes0 = keep.tile([P, S], U32, align_bytes=64, name="x_codes0")
        x_scales0 = keep.tile([P, S], U8, align_bytes=64, name="x_scales0")
        x_woven0 = keep.tile([P, S, PACK], BF16, align_bytes=64, name="x_woven0")
        picked0 = keep.tile([P, PACK, S], F32, name="picked0")
        for t in range(PACK):
            gather = nc.vector.tensor_copy if t % 2 == 0 else scalar_gather
            gather(picked0[:, t, :], picked_from(rows[t], 0, S))
        cut = 2 * THIRD
        weave_all(nc.vector.tensor_copy, x_woven0[:, 0:cut, :], picked0[:, :, 0:cut])
        nc.scalar.activation(
            x_woven0[:, cut:S, :], picked0[:, :, cut:S].rearrange("p t n -> p n t"), IDENTITY, bias=gelu_zero[:]
        )
        for a, b in ((0, cut), (cut, S)):
            quantise(x_codes0[:, a:b], x_scales0[:, a:b], flat(x_woven0[:, a:b, :]))

        thirds = [slice(i * THIRD, (i + 1) * THIRD) for i in range(3)]
        picked1 = keep.tile([P, PACK, S], F32, name="picked1")
        x_woven1 = [keep.tile([P, THIRD, PACK], BF16, align_bytes=64, name=f"x_woven1{i}") for i in range(2)]
        x_codes1 = []
        x_scales1 = keep.tile([P, S], U8, align_bytes=64, name="x_scales1")

        def weave_pair(copy, i, t):
            copy(x_woven1[i][:, :, t : t + 2], picked1[:, t : t + 2, thirds[i]].rearrange("p t n -> p n t"))

        nc.vector.tensor_copy(picked1[:, 0, :], picked_from(rows[4], 0, S))
        scalar_gather(picked1[:, 1, :], picked_from(rows[5], 0, S))
        weave_pair(nc.vector.tensor_copy, 0, 0)
        nc.vector.tensor_copy(x_woven1[0][:, :, 2], picked_from(rows[6], 0, THIRD))
        scalar_gather(picked1[:, 2, THIRD:S], picked_from(rows[6], THIRD, S))

        w1_codes = [keep.tile([P, H], U32, align_bytes=64, name=f"w1_codes{s}") for s in range(PASSES)]
        w1_scales = [keep.tile([P, H], U8, align_bytes=64, name=f"w1_scales{s}") for s in range(PASSES)]
        w1_woven = [
            [
                keep.tile([P, 2, P, PACK], BF16, align_bytes=64, name=f"w1_woven{s}{pair}", tag=f"w1_woven{s}{pair}")
                for pair in range(2)
            ]
            for s in range(PASSES)
        ]

        def weave_w1(s, pair, raw, share):
            dst = w1_woven[s][pair][:].rearrange("p t m j -> p m j t")
            src = raw[:].rearrange("p j (m t) -> p m j t", t=PACK)[:, :, :, 2 * pair : 2 * pair + 2]
            nc.vector.tensor_copy(dst[:, 0:share], src[:, 0:share])
            nc.scalar.copy(dst[:, share:P], src[:, share:P])

        def quantise_w1(s, a, b):
            woven = w1_woven[s][a // 2][:, a % 2 : a % 2 + b - a].rearrange("p t m j -> p (t m j)")
            quantise(w1_codes[s][:, P * a : P * b], w1_scales[s][:, P * a : P * b], woven)

        def quantise_third(i, woven, tag):
            codes = keep.tile([P, THIRD], U32, align_bytes=64, name=f"x_codes1{i}", tag=tag)
            quantise(codes[:], x_scales1[:, thirds[i]], flat(woven[:]))
            x_codes1.append(codes)

        for pair in range(2):
            weave_w1(0, pair, w1_raw0, M_PASS0)
        for pair in range(2):
            quantise_w1(0, 2 * pair, 2 * pair + 2)

        nc.vector.tensor_copy(x_woven1[0][:, :, 3], picked_from(rows[7], 0, THIRD))
        for i in (1, 2):
            scalar_gather(picked1[:, 3, thirds[i]], picked_from(rows[7], thirds[i].start, thirds[i].stop))
        quantise_third(0, x_woven1[0], "x_codes10")
        weave_all(nc.vector.tensor_copy, x_woven1[1][:], picked1[:, :, thirds[1]])
        x_woven_last = [keep.tile([P, SLICE, PACK], BF16, align_bytes=64, name="x_woven4")]
        weave_all(nc.scalar.copy, x_woven_last[0][:], picked1[:, :, 4 * SLICE : 5 * SLICE])

        for pair in range(2):
            weave_w1(1, pair, w1_raw1, M_LATE)
        for t in range(PACK):
            quantise_w1(1, t, t + 1)
        quantise_third(1, x_woven1[1], "w1_woven10")
        x_woven_last.append(keep.tile([P, SLICE, PACK], BF16, align_bytes=64, name="x_woven5", tag="last_raw"))
        weave_all(nc.vector.tensor_copy, x_woven_last[1][:], picked1[:, :, 5 * SLICE : S])
        x_codes1.append(keep.tile([P, THIRD], U32, align_bytes=64, name="x_codes12", tag="w1_woven11"))
        for i in range(2):
            cols = slice((4 + i) * SLICE, (5 + i) * SLICE)
            quantise(x_codes1[2][:, i * SLICE : (i + 1) * SLICE], x_scales1[:, cols], flat(x_woven_last[i][:]))

        w2_woven = keep.tile([P, N, PACK], BF16, align_bytes=64, name="w2_woven")
        w2_codes = keep.tile([P, N], U32, align_bytes=64, name="w2_codes")
        w2_scales = keep.tile([P, N], U8, align_bytes=64, name="w2_scales")
        weave_all(nc.vector.tensor_copy, w2_woven[:], w2_raw[:])
        quantise(w2_codes[:], w2_scales[:], flat(w2_woven[:]))


        def x_codes(s, cols):
            if s == 0:
                return x_codes0[:, cols]
            first = cols.start // THIRD * THIRD
            return x_codes1[cols.start // THIRD][:, cols.start - first : cols.stop - first]

        x_scales = (x_scales0, x_scales1)

        def layer1(dst, s, t, cols, start, stop):
            nc.tensor.matmul_mx(
                out=dst,
                lhsT=w1_codes[s][:, t * P : (t + 1) * P].bitcast(FP8X4),
                lhsT_scale=w1_scales[s][:, t * P : (t + 1) * P],
                rhs=x_codes(s, cols).bitcast(FP8X4),
                rhs_scale=x_scales[s][:, cols],
                start=start,
                stop=stop,
            )

        batches = ((0, 256, "acc0"), (256, 512, "acc1"), (512, 640, "acc2"), (640, 704, "acc3"), (704, 768, "acc4"))
        h = {
            a: keep.tile([P, b - a, PACK], BF16, align_bytes=64, name=f"h{a}", tag=f"h{a}") for a, b, tag in batches
        }

        def h_part(a, b):
            first = max(start for start in h if start <= a)
            return h[first][:, a - first : b - first, :]

        h_rows = keep.tile([P, PACK, THIRD], BF16, align_bytes=64, name="h_rows")
        groups = ((0, 1), (1, 2), (2, 3), (3, 4))
        early = [banks.tile([P, b - a, THIRD], F32, name=f"early{a}", tag=f"acc{g}") for g, (a, b) in enumerate(groups)]
        for s in range(PASSES):
            for g, (a, b) in enumerate(groups):
                for t in range(a, b):
                    layer1(early[g][:, t - a, :], s, t, thirds[0], s == 0 and t == a, s == 1 and t == b - 1)
        for g, (a, b) in enumerate(groups):
            nc.scalar.activation(h_rows[:, a:b, :], early[g][:], GELU)
        weave_all(nc.vector.tensor_copy, h_part(0, THIRD), h_rows[:])

        for i, tag in ((2, "acc4"), (3, "acc5"), (4, "acc6"), (5, "acc7")):
            cols = slice(i * SLICE, (i + 1) * SLICE)
            acc = banks.tile([P, PACK, SLICE], F32, name=f"acc_slice{i}", tag=tag)
            for s in range(PASSES):
                for t in range(PACK):
                    layer1(acc[:, t, :], s, t, cols, s == 0 and t == 0, s == 1 and t == PACK - 1)
            pieces = ((0, SLICE),) if i < SLICES - 1 else ((0, SLICE // 2), (SLICE // 2, SLICE))
            for a, b in pieces:
                nc.scalar.activation(
                    h_part(i * SLICE + a, i * SLICE + b), acc[:, :, a:b].rearrange("p t n -> p n t"), GELU
                )

        h_codes = keep.tile([P, S], U32, align_bytes=64, name="h_codes")
        h_scales = keep.tile([P, S], U8, align_bytes=64, name="h_scales")
        y_parts = []
        for a, b, tag in batches:
            quantise(h_codes[:, a:b], h_scales[:, a:b], flat(h_part(a, b)))
            y_part = banks.tile([P, b - a], F32, name=f"y_part{a}", tag=tag)
            nc.tensor.matmul_mx(
                out=y_part[:],
                lhsT=w2_codes[:].bitcast(FP8X4),
                lhsT_scale=w2_scales[:],
                rhs=h_codes[:, a:b].bitcast(FP8X4),
                rhs_scale=h_scales[:, a:b],
                start=True,
                stop=True,
            )
            y_parts.append(y_part)
        y = keep.tile([P, S], F32, align_bytes=64, name="y", tag="h704")
        for i, (a, b, tag) in enumerate(batches):
            copy = nc.scalar.copy if i % 2 == 0 else nc.vector.tensor_copy
            copy(y[:, a:b], y_parts[i][:])

        blocks = [slice(i * P, (i + 1) * P) for i in range(V // P)]
        fetched = keep.tile([P, D - 1, V], F32, name="fetched")
        terms = [keep.tile([P, V], F32, name=f"term{d}") for d in range(D)]
        pair = keep.tile([P, V], F32, name="pair")
        total = keep.tile([P, V], F32, name="total")

        def looked_up(d, b):
            return y[:].indirect(places[d][:, blocks[b].start // 16 : blocks[b].stop // 16])

        for d, b in ((2, 0), (1, 1), (2, 1), (1, 2), (2, 2)):
            nc.scalar.activation(fetched[:, d - 1, blocks[b]], looked_up(d, b), COPY)
        nc.vector.tensor_tensor(terms[1][:, blocks[0]], looked_up(1, 0), gates[:, 1, blocks[0]], MULT)
        nc.vector.tensor_tensor(terms[0][:], y[:].indirect(places[0][:]), gates[:, 0, :], MULT)

        def weigh(d, b):
            nc.vector.tensor_mul(terms[d][:, blocks[b]], fetched[:, d - 1, blocks[b]], gates[:, d, blocks[b]])

        def add_pair(b):
            nc.vector.tensor_add(pair[:, blocks[b]], terms[0][:, blocks[b]], terms[1][:, blocks[b]])

        def add_third(b):
            nc.vector.tensor_add(total[:, blocks[b]], pair[:, blocks[b]], terms[2][:, blocks[b]])

        weigh(2, 0)
        weigh(1, 1)
        add_pair(0)
        weigh(2, 1)
        add_pair(1)
        weigh(1, 2)
        add_third(0)
        weigh(2, 2)
        add_pair(2)
        add_third(1)
        add_third(2)
        nc.sync.dma_start(out, total[:])
